import numpy as np, ml_dtypes
CORES = [6,15,38,47]
N = 4
import mx_ref
BF = ml_dtypes.bfloat16
def gentries(a):
    return np.ascontiguousarray(a.reshape(8, 16, -1).transpose(0, 2, 1)).reshape(8, -1)
def gtable(e):
    e = np.asarray(e); return np.ascontiguousarray(e.reshape(8, -1, 16).transpose(0, 2, 1)).reshape(128, -1).astype(np.int32)
def gcols(t, e):
    v = np.concatenate([t.reshape(8, 16, -1, 4), np.zeros((8, 16, 1, 4), BF)], axis=2)
    return np.ascontiguousarray(np.stack([v[g][:, e[g]] for g in range(8)])).reshape(128, -1)
def tile(rs):
    return np.stack(rs, axis=2).reshape(128, -1).astype(BF)
def pick(q, e):
    c = np.concatenate([q[0].reshape(128, -1, 4), np.zeros((128, 1, 4), np.uint8)], axis=1); s = np.concatenate([q[1], np.ones((16, 1), np.uint8)], axis=1)
    return (np.ascontiguousarray(c[:, e].reshape(128, -1)), np.ascontiguousarray(s[:, e]))
def join(*qs):
    return (np.concatenate([q[0] for q in qs], axis=1), np.concatenate([q[1] for q in qs], axis=1))
def put(q, e, v):
    c, s = q[0].reshape(128, -1, 4).copy(), q[1].copy(); c[:, e] = v[0].reshape(128, -1, 4); s[:, e] = v[1]
    return (c.reshape(128, -1), s)
def pk(c, s):
    return (np.ascontiguousarray(c), mx_ref.live(s))
def emit(q):
    return q[0], q[1]
def packed(v, rng):
    q = [mx_ref.quantize(np.ascontiguousarray(v[r])) for r in range(N)]
    return np.stack([a for a, b in q]), np.stack([mx_ref.plane(b, rng) for a, b in q])
def values_of_codes():
    e, c = np.zeros((128, 128, 4), np.float32), np.zeros((128, 2, 4), np.uint8)
    e[np.arange(128), np.arange(128), 0] = 1
    c[:127, :, 0] = np.arange(256).reshape(2, 128).T[:127]
    return mx_ref.matmul(mx_ref.quantize(e.reshape(128, 512).astype(BF)), (c.reshape(128, 8), np.full((16, 2), 127, np.uint8))).T.reshape(-1).astype(np.float64)
CODE_VALUE, SCALE_VALUE = values_of_codes(), 2.0 ** (np.arange(256) - 127.0)
def decode(q):
    return (CODE_VALUE[q[0]].reshape(16, 8, -1, 4) * SCALE_VALUE[q[1]][:, None, :, None] + 0.0).reshape(128, -1).astype(np.float32)
def f(rng, *shape):
    return mx_ref.flush((rng.standard_normal(shape, dtype=np.float32) * np.exp2(rng.integers(-2, 3, shape[:-1] + (1,)))).astype(BF))
def wide(rng, *shape, cols=0):
    v = rng.standard_normal(shape, dtype=np.float32) * np.exp2(rng.integers(-12, 13, shape)).astype(np.float32)
    if cols: v *= np.repeat(np.exp2(rng.integers(-cols, cols + 1, shape[:-2] + (1, shape[-1] // 4))) * (rng.random(shape[:-2] + (1, shape[-1] // 4)) > 0.0625), 4, axis=-1).astype(np.float32)
    return mx_ref.flush(v.astype(BF))
C, E, B, R = 320, 20, 112, 2
L = C + B
M = L - 2 * E - 15
S = np.arange(16)
AT = np.arange(0, E, E // 4)
G = np.arange(8)[:, None, None]
def choose(s, b):
    p, n = b.copy(), b.copy()
    for k in range(1, 16):
        n[:, k] = p[:, k - 1] + E
        c = b[:, k:k + 1] + S
        d = np.max(np.abs(s[G, n[:, k, None, None] + AT] - s[G, c[:, :, None] + AT]), axis=2)
        d[c == n[:, k:k + 1]] = np.inf
        p[:, k] = b[:, k] + np.argmin(d, axis=1)
    return p, n
def places(e):
    return (e[:, :, None] + np.arange(E)).reshape(8, C)
def big(v):
    v = v.astype(np.float32)
    v[np.abs(v) < np.float32(2.0 ** -16)] = 0
    return v.astype(BF)
def numbers_of(rng):
    return {"x": big(f(rng, N, 128, 4 * C)), "u": np.array(f(rng, N, 128, 512)), "v": np.array(f(rng, N, 128, 512))}
def lists_of(rng):
    hop = rng.integers(E - E // 4, E + E // 4 + 1, (N, 8, R, 1))
    return (hop * S + rng.integers(0, M - 15 * (E + E // 4) + 1, (N, 8, R, 16))).reshape(N, 8, 16 * R)
def even(rng, k):
    return (rng.integers(0, M - 15 * E + 1, (k, R, 1)) + E * S).reshape(k, 16 * R)
def halves(rng, k):
    return rng.integers(0, C // 2 - 15 - 2 * E + 1, (k, 16)) + C // 2 * (S % 2)
def stored(l):
    return np.stack([gtable(e) for e in l])
def weights(rng, w):
    c, p = packed(w, rng)
    return {"wc": c, "ws": p}
def layers(rng):
    return weights(rng, f(rng, N, 128, 2048))
def unit(rng, a):
    w = np.zeros((N, 128, 4, 128, 4), np.float32)
    i = np.arange(128)
    for b in range(4): w[:, i, b, i, b] = a
    return weights(rng, w.reshape(N, 128, 2048).astype(BF))
def setup_inputs(rng):
    return {**numbers_of(rng), "st": stored(lists_of(rng)), **layers(rng)}
def setup_inputs_ties(rng):
    d, l = numbers_of(rng), lists_of(rng)
    o = rng.permutation(N)
    x = d["x"].reshape(N, 8, 16, C, 4)
    for r in range(N):
        k = np.zeros(C, int) if r == o[0] else rng.permutation(C) % 3
        a = x[r][:, :8, :3].copy()
        a[:, :, 2] = 0
        x[r][:, :8] = a[:, :, k]
    x[o[1]] = 0
    l[o[0], :2] = even(rng, 2)
    l[o[1], 0] = rng.integers(C, M + 1, 16 * R)
    u = d["u"].reshape(N, 8, 16, 128, 4)
    u[:, :, 8:, ::16] = 0
    return {"x": x.reshape(N, 128, 4 * C), "u": u.reshape(N, 128, 512), "v": d["v"], "st": stored(l), **layers(rng)}
def setup_inputs_near(rng):
    d, l = numbers_of(rng), lists_of(rng)
    o = rng.permutation(N)
    h, j = C // 2, np.arange(C)
    sign, t, tiny = np.ones((N, 8, C)), np.zeros((N, C), int), []
    for r in range(N):
        t[r] = np.where(j < h, h - 1 - j, j - h) if o[r] % 4 < 2 else rng.integers(0, 256, C)
        far = rng.permutation(8) % 2 == 1
        sign[r] = np.where(far[:, None] & (j >= h), -1.0, 1.0)
        l[r, far, :16] = halves(rng, 4)
        if o[r] % 4 == 1:
            e = rng.permutation(np.flatnonzero(~far))[:2]
            l[r, e, :16] = halves(rng, 2)
            tiny += [(r, int(i)) for i in e]
    g = ((t[:, :, None] >> np.arange(8)) & 1) * np.exp2(np.arange(8) - 23.0)
    x = d["x"].astype(np.float32).reshape(N, 8, 16, C, 4)
    x[:, :, 0] = 0
    x[:, :, 0, :, 0] = sign
    x[:, :, 8] = g[:, None, :, :4]
    x[:, :, 9] = g[:, None, :, 4:]
    x[:, :, 10:] = rng.integers(4, 8, (N, 8, 6, C, 4)) * rng.choice([-1.0, 1.0], (N, 8, 6, C, 4)) * 2.0 ** -20
    x *= np.where(o % 2, 2.0 ** -4, 1.0).astype(np.float32)[:, None, None, None, None]
    u = d["u"].reshape(N, 128, 128, 4)
    k = np.where(o % 2, 2.0 ** -30, 1.0).astype(np.float32).astype(BF)
    u[:, :, ::16] = 0
    for i in range(0, 128, 16):
        u[:, i, i, 0] = k
        u[:, i + 8:i + 10, i] = k[:, None, None]
    for r, i in tiny:
        w = t[r] // 8 + 32 * (j < h)
        x[r, i, :8] = 0
        x[r, i, 1, :, 0] = (8 + w % 8) * 2.0 ** -32
        x[r, i, 2, :, 0] = (8 + w % 8) * 2.0 ** -32
        x[r, i, 3, :, 0] = (8 + w // 8) * 2.0 ** -32
        u[r, :, 16 * i] = 0
        u[r, 16 * i + 1:16 * i + 4, 16 * i, 0] = (np.array([-1.0, 1.125, 1.0]) * 2.0 ** -30).astype(np.float32).astype(BF)
    return {"x": x.reshape(N, 128, 4 * C).astype(BF), "u": u.reshape(N, 128, 512), "v": d["v"], "st": stored(l), **unit(rng, 32)}
def setup_inputs_huge(rng):
    d, l = numbers_of(rng), lists_of(rng)
    o = rng.permutation(N)
    a = np.zeros((N, C))
    m = 0.9 + 0.1 * rng.random((N, 128, C, 4))
    k = 0.9 + 0.1 * rng.random((N, 128, 8, 4))
    for r in range(N):
        if o[r] % 2:
            l[r, :, :16] = even(rng, 8)[:, :16]
            if o[r] % 4 == 1:
                i = int(l[r, 0, 1])
                a[r] = rng.choice([-1.0, 1.0], C)
                a[r, i] = 1
                a[r, i + 1:i + 16] = -1
                m[r, :, i:i + 16] = 1
                k[r] = 1
            else:
                a[r] = rng.uniform(-1, 1, C)
        else:
            a[r] = np.where(np.arange(C) < C // 2, 1.0, -1.0)
            l[r, :, :16] = halves(rng, 8)
    x = 2.0 ** 30 * m * a[:, None, :, None]
    g = np.stack([rng.permutation(8) % 2 * 2.0 - 1.0 for r in range(N)])
    u = d["u"].reshape(N, 128, 128, 4)
    u[:, :, ::16] = (2.0 ** 30 * k * g[:, None, :, None]).astype(np.float32).astype(BF)
    return {"x": x.astype(np.float32).reshape(N, 128, 4 * C).astype(BF), "u": u.reshape(N, 128, 512), "v": d["v"], "st": stored(l), **unit(rng, -16)}
def setup_inputs_lists(rng):
    d, l = numbers_of(rng), lists_of(rng)
    for r in range(N):
        g = rng.permutation(8)
        l[r, g[:2]] = rng.integers(0, M + 1, (2, 16 * R))
        l[r, g[2:4]] = M
        l[r, g[4]] = np.sort(rng.integers(0, M + 1, (R, 16)), axis=1)[:, ::-1].reshape(-1)
        l[r, g[5]] = even(rng, 1)[0]
        l[r, g[6]] = rng.integers(C, M + 1, 16 * R)
        l[r, g[7]] = 0
    return {**d, "st": stored(l), **layers(rng)}
def setup_inputs_spread(rng):
    d = setup_inputs(rng)
    d["x"] = big(wide(rng, N, 128, 4 * C, cols=6))
    return d
def check_inputs(d):
    b = []
    for k in ("x", "u", "v"):
        a = np.abs(d[k].astype(np.float32))
        if not (np.isfinite(a).all() and ((a == 0) | (a >= 2.0 ** -30) & (a <= 2.0 ** 30)).all()): b.append("a value of " + k)
    if ((d["st"] < 0) | (d["st"] > M)).any(): b.append("an entry of st")
    return b
def reference(x, u, v, st, wc, ws):
    qu = [mx_ref.quantize(u[r]) for r in range(N)]
    lay = [pk(wc[r], ws[r]) for r in range(N)]
    first = [gentries(st[r]).astype(np.int64) for r in range(N)]
    now = [x[r] for r in range(N)]
    y, ol = np.zeros((N, 128, C), np.float32), np.zeros((N, 8, 16 * R), np.float32)
    oc, osc = np.zeros((N, 128, 4 * C), np.uint8), np.zeros((N, 16, C), np.uint8)
    for t in range(R):
        q = [mx_ref.quantize(now[r]) for r in range(N)]
        now = []
        for r in range(N):
            window = join(q[r], pick(q[(r + 1) % N], np.arange(B)))
            p, n = choose(mx_ref.matmul(qu[r], window)[::16], first[r][:, 16 * t:16 * t + 16])
            ol[r, :, 16 * t:16 * t + 16] = p
            d = decode(window).astype(BF)
            z = (gcols(d, places(n)).astype(np.float32) + gcols(d, places(p)).astype(np.float32)) * np.float32(0.5)
            qz = mx_ref.quantize(z.astype(BF))
            w = lay[(r + 1 + t) % N]
            h = tile([mx_ref.matmul(pick(w, np.arange(128 * b, 128 * b + 128)), qz) * np.float32(0.03125) for b in range(4)])
            now.append((decode(qz) + decode(mx_ref.quantize(h))).astype(BF))
    for r in range(N):
        q = mx_ref.quantize(now[r])
        y[r] = mx_ref.matmul(mx_ref.quantize(v[r]), q)
        oc[r], osc[r] = emit(q)
    return {"y": y, "ol": ol, "oc": oc, "osc": osc}

@@ -1,0 +1,402 @@
+from concourse.mybir import dt, AluOpType, ActivationFunctionType
+
+C, E, B, R = 320, 20, 112, 2
+L = C + B
+K = 15
+CUT = (128, 192)
+FINE = ((0, 2, 6, 11, 15), (0, 2, 5, 9, 12, 15))
+COARSE = ((0, 6, 11, 15), (0, 5, 9, 15))
+PICKS = ((0, 32, 80, 128, 192, 256, 320), (0, 48, 96, 144, 192, 256, 320))
+PIECE = (((0, C, 0), (L - 128, L, C)), ((0, CUT[0], 0), (CUT[0], L, CUT[0])))
+HEAD = 128
+ORDER = "G8 V9 V13 V10 V11 V12 V14 V85 V18 Y1 Y0 Y2 Y3 V86 G29 V48 S17 G21 Y4 S16 V22 V30 G62 Y5 V28 G63 G103 V68 V102 G104 S6 V19 V58 S65 V66 S59 V32 V60 V33 V61 S20 G105 Y7 V15 V64 G49 G25 G23 G31 G107 G108 G34 G35 G39 V69 V54 S56 S83 V27 V55 S70 V110 P111 V67 S81 S78 S93 S94 S91 V71 S77 V73 V89 V53 V79 S80 S76 S112 V50 P113 S114 V90 V26 S95 V74 V75 S87 G40 G47 V52 V51 P115 V116 V96 V82 G36 P117 V84 V24 S118 V92 V97 A106 G37 G41 G42 P125 V57 P123 S126 P119 V124 S135 P121 P129 S150 S145 S44 G98 V140 V136 V141 V72 V142 S143 V137 V151 A109 S138 V146 S120 V144 V139 V155 V45 S130 V156 P127 V157 S158 V147 V159 V170 V46 V171 S148 S122 V152 V172 V149 V173 V160 V174 S128 V161 V175 S38 S153 V88 P133 V185 V162 P131 V186 S132 V187 V154 S134 G99 S163 S190 V164 V165 V176 V166 V177 S192 S188 V167 V191 V193 V189 S43 V178 V194 V179 S168 P197 P195 P196 V169 V180 V181 P198 P201 V182 S205 P202 V183 P200 S203 S204 V184 P199 V206 V235 V207 P210 P209 V236 P208 S214 V237 V212 S242 P211 V213 V215 V216 V243 S240 V241 P229 G217 P223 P227 P225 S238 S226 S228 V239 G218 V244 S224 P231 P233 S230 S232 S234 P247 P248 P245 V100 V267 V256 S255 P246 S253 V254 P249 P252 P251 V257 P250 P258 P261 V265 S262 P259 P260 V264 S263 V266 V101 A219 P270 P268 V269 S271 V290 V291 P272 S285 S280 V286 G220 S295 V281 G221 V287 V282 S273 S288 S283 P274 V292 S300 P278 V289 V284 V296 V305 S293 V306 V301 V307 V297 V302 V294 S308 S298 V309 V310 S303 V299 V311 V320 V304 P276 S277 V312 V315 V321 V316 S313 V322 V317 S318 V323 V314 V324 V325 V326 V327 V319 V328 V329 S279 V335 V330 V336 V331 V337 V332 V333 V334 V370 S275 S340 S338 S342 V371 V341 S344 V372 V339 V343 S375 V345 S373 V346 V376 V374 V377 V401 A222 P349 P348 P347 P352 P350 P354 P351 S357 S356 S355 S358 P353 P380 P379 P378 P381 S402 V359 S388 P361 V387 P363 S386 S389 S367 V365 P360 V390 P362 V366 P383 P392 P385 S364 V368 P382 P384 S369 P393 S397 P403 P394 V396 S398 V404 P391 V395 S405 V399 P406 S400 Y412 S409 Y410 V407 S408 Y411"
+Q4, U8, F32, BF, I32, U16 = "float8_e4m3fn_x4", "uint8", "float32", "bfloat16", "int32", "uint16"
+
+SCRATCH = {}
+for _n, _w, _d in (("xin", 4 * C, BF), ("uin", 512, BF), ("vin", 512, BF), ("sti", 2, I32), ("wq", 512, Q4),
+                   ("wp", 512, U8), ("uq", 128, Q4), ("up", 128, U8), ("urq", 256, Q4), ("urp", 256, U8),
+                   ("nq", 128, Q4), ("npl", 128, U8), ("ones", 516, BF), ("ef", 516, BF), ("eq", 512, Q4),
+                   ("ep", 512, U8), ("pi", 2, I32), ("ai", 8, I32), ("af", 16, F32), ("io40", 40, F32),
+                   ("wpen", 40, F32), ("t20", 48, F32), ("lf", 112, F32), ("upo", 16, U16), ("off", 96, U16),
+                   ("kli", 20, I32), ("klf", 20, F32), ("kl", 20, U16), ("kt", 16 * K, BF), ("rst", 16 * K, F32),
+                   ("stf", 2, F32), ("bb", 64, F32), ("bt", 64, F32), ("lb", 8, F32), ("bs", 48, F32),
+                   ("bd", 48, F32), ("db", 40, F32), ("po", 40, U16), ("jf", 48, F32), ("pm", 512, F32),
+                   ("pout", 32, F32), ("ysb", C, F32), ("vq2", C, Q4), ("vp2", C, U8)):
+    SCRATCH[_n] = ("sbuf", [128, _w], _d)
+for _t in range(R):
+    for _n, _w, _d in (("vq", L, Q4), ("vp", L, U8), ("lq", 512, Q4), ("lp", 512, U8), ("sc", 2 * L, F32),
+                       ("dv", 4 * L, F32), ("tf", 8 * K, F32), ("tl", 8 * K, U16), ("pen", 64 * K, BF),
+                       ("ut", C // 2, F32), ("lc", C // 2, F32), ("l2", C // 2, F32), ("li", C // 2, U16),
+                       ("tp", 64 * K, F32), ("tb", 64 * K, F32), ("dd", 64 * K, F32), ("aa", 64 * K, F32),
+                       ("s1", 64 * K, F32), ("nr", 16 * K, BF), ("s3", 16 * K, BF), ("bc", 32 * K, BF),
+                       ("rr", 32 * K, BF), ("ch", 16 * K, U16), ("zn", 4 * C, F32), ("zt", 4 * C, BF), ("zq", C, Q4),
+                       ("zp", C, U8), ("ht", 4 * C, BF), ("hq", C, Q4), ("hp", C, U8), ("xt", 4 * C, BF)):
+        SCRATCH["%s%d" % (_n, _t)] = ("sbuf", [128, _w], _d)
+for _b in range(8):
+    SCRATCH["ps%d" % _b] = ("psum", [128, 512], F32)
+SEMAPHORES = ["cV", "cS", "cP", "cG", "sent", "win0", "win1", "lay0", "lay1"] + ["d%d" % i for i in range(20)]
+
+ALU, ACT = AluOpType, ActivationFunctionType
+
+
+def build(g, T, topo, core):
+    ops = []
+    cores, rank = T.cores, T.rank_of(core)
+    n_r = len(cores)
+    queue = {"S": g.scalar, "Y": g.sync}
+
+    def ap(r):
+        return T[r[0]][:, r[1]:r[2]] if len(r) == 3 else T[r[0]][:, r[1]:r[2]:r[3]]
+
+    def cnt(r):
+        return len(range(*r[1:]))
+
+    def add(on, size, reads, writes, emit, **kw):
+        o = dict(on=on, size=size, reads=[x for x in reads if isinstance(x, tuple)], writes=writes, emit=emit,
+                 after=[], kind="op")
+        o.update(kw)
+        ops.append(o)
+        return len(ops) - 1
+
+    def kind(ind, o, *rs):
+        two = all(SCRATCH[r[0]][2] in (BF, U16) for r in (o,) + rs)
+        return ("pick" if ind else "half" if two else "one", cnt(o))
+
+    def src(i, ind):
+        return ap(i) if ind is None else ap(i).indirect(ap(ind))
+
+    def scal(s):
+        return ap(s) if isinstance(s, tuple) else s
+
+    def copy(o, i, ind=None, scale=None, bias=None):
+        whole = SCRATCH[o[0]][2] in (U16, I32) or SCRATCH[i[0]][2] in (U16, I32)
+
+        def emit(e):
+            if e == "S":
+                kw = {}
+                if scale is not None:
+                    kw["scale"] = scal(scale)
+                if bias is not None:
+                    kw["bias"] = scal(bias)
+                return g.scalar.activation(ap(o), src(i, ind), ACT.Copy if bias is None else ACT.Identity, **kw)
+            if scale is None and bias is None:
+                return g.vector.tensor_copy(ap(o), src(i, ind))
+            if bias is None:
+                return g.vector.tensor_scalar(ap(o), src(i, ind), scal(scale), None, ALU.mult)
+            if scale is None:
+                return g.vector.tensor_scalar(ap(o), src(i, ind), scal(bias), None, ALU.add)
+            return g.vector.tensor_scalar(ap(o), src(i, ind), scal(scale), scal(bias), ALU.mult, ALU.add)
+        return add("V" if whole else "VS", kind(ind, o, i), [i, ind, scale, bias], [o], emit)
+
+    def absol(o, i, ind):
+        return add("S", kind(ind, o, i), [i, ind], [o], lambda e: g.scalar.activation(ap(o), src(i, ind), ACT.Abs))
+
+    def ts(o, i, s1, op0, s2=None, op1=None, ind=None):
+        def emit(e):
+            if op1 is None:
+                return g.vector.tensor_scalar(ap(o), src(i, ind), scal(s1), None, op0)
+            return g.vector.tensor_scalar(ap(o), src(i, ind), scal(s1), scal(s2), op0, op1)
+        return add("V", kind(ind, o, i), [i, ind, s1, s2], [o], emit)
+
+    def tt(o, a, b, op, ind=None):
+        return add("V", ("pick" if ind else "two", cnt(o)), [a, b, ind], [o],
+                   lambda e: g.vector.tensor_tensor(ap(o), src(a, ind), ap(b), op))
+
+    def scan(o, a, b, op0, op1):
+        return add("V", kind(None, o, a, b), [a, b], [o],
+                   lambda e: g.vector.tensor_tensor_scan(ap(o), ap(a), ap(b), 0.0, op0, op1))
+
+    def turn(o, i):
+        return add("V", kind(None, o, i), [i], [o], lambda e: g.vector.transpose(ap(o), ap(i)))
+
+    def fill(o, c):
+        return add("V", kind(None, o), [], [o], lambda e: g.vector.memset(ap(o), c))
+
+    def iota(o, pat, base, cm=0):
+        def emit(e):
+            if SCRATCH[o[0]][2] == I32:
+                return g.iota(ap(o), pat, base, cm)
+            return g.iota(ap(o), pat, base, cm, allow_small_or_imprecise_dtypes=True)
+        return add("G", ("pool", cnt(o)), [], [o], emit)
+
+    def select(o, i, pat, op, other, base, cm):
+        return add("G", ("pool", cnt(o)), [i], [o], lambda e: g.affine_select(ap(o), ap(i), pat, op, other, base, cm))
+
+    def quant(q, a, b, i):
+        c, p = (q[0], a, b), (q[1], a, b)
+        return add("V", ("quant", cnt(i)), [i], [c, p], lambda e: g.vector.quantize_mx(ap(c), ap(p), ap(i)))
+
+    def mm(bank, w, x, a, b, wa=0, start=True, stop=True):
+        wq_, wp_, xq_, xp_ = (w[0], wa, wa + 128), (w[1], wa, wa + 128), (x[0], a, b), (x[1], a, b)
+        o = ("ps%d" % bank, 0, b - a)
+        return add("P", ("mm", b - a), [wq_, wp_, xq_, xp_], [o],
+                   lambda e: g.tensor.matmul_mx(ap(o), ap(wq_), ap(wp_), ap(xq_), ap(xp_), start, stop), acc=not start)
+
+    ndma = [0]
+
+    def dma(out, in_, reads, writes, size):
+        ndma[0] += 1
+        return add("YS", ("dma", size), reads, writes, lambda e: queue[e].dma_start(out, in_),
+                   kind="dma", sem="d%d" % (ndma[0] - 1))
+
+    def u8(r):
+        return ap(r).bitcast(dt.uint8)
+
+    sends = []
+
+    def send(step, s, d, sem):
+        dst = cores[(rank - step) % n_r]
+        rid, pid, _ = topo.addr(dst)
+        codes = SCRATCH[s[0]][2] == Q4
+        sends.append(add("G", ("send", cnt(s) * (4 if codes else 1)), [s], [],
+                         lambda e: g.remote_dma(u8(d) if codes else ap(d), u8(s) if codes else ap(s), T.sem[sem],
+                                                T.sem.sent, pid, rid, topo.mask(core, dst)),
+                         kind="send", inc=len(topo.engines(core, dst)), after=sends[-1:]))
+
+    def arrival(step, lands, sem):
+        add("A", ("arrive", 0), [], lands, None, kind="arrive", sem=sem, after=sends[-1:],
+            inc=len(lands) * len(topo.engines(cores[(rank + step) % n_r], core)))
+
+    a0 = 4 * 128
+    dma(T.xin[:, 0:a0], T.x[:, 0:a0], [], [("xin", 0, a0)], 2 * a0)
+    dma(T.wp[:, 0:HEAD], T.ws[:, 0:HEAD], [], [("wp", 0, HEAD)], HEAD)
+    dma(T.sti[:], T.st[:], [], [("sti", 0, 2)], 8)
+    dma(T.uin[:], T.u[:], [], [("uin", 0, 512)], 1024)
+    dma(T.xin[:, a0:4 * C], T.x[:, a0:4 * C], [], [("xin", a0, 4 * C)], 8 * C - 2 * a0)
+    dma(T.wp[:, HEAD:512], T.ws[:, HEAD:512], [], [("wp", HEAD, 512)], 512 - HEAD)
+    dma(u8(("wq", 0, 512)), T.wc[:], [], [("wq", 0, 512)], 2048)
+    dma(T.vin[:], T.v[:], [], [("vin", 0, 512)], 1024)
+
+    iota(("pi", 0, 1), [[0, 1]], 0, 1)
+    for j, m in enumerate((15, 16, 3, None, 31)):
+        if m is None:
+            ts(("ai", j, j + 1), ("pi", 0, 1), 2, ALU.arith_shift_right, 3, ALU.bitwise_and)
+        else:
+            ts(("ai", j, j + 1), ("pi", 0, 1), m, ALU.bitwise_and)
+    copy(("af", 0, 5), ("ai", 0, 5))
+    col = lambda j: ("af", j, j + 1)
+    c_r, c_h, c_tl, c_cl, c_pm, c_r4, c_kl, c_j = col(0), col(1), col(6), col(7), col(8), col(9), col(10), col(11)
+    ts(c_tl, c_h, 5.0 / 16, ALU.mult, c_r, ALU.subtract)
+    copy(c_cl, c_h, scale=L / 16.0, bias=c_r)
+    copy(c_pm, col(2), scale=16.0, bias=col(3))
+    copy(c_r4, c_r, scale=0.25)
+    copy(c_kl, c_r, scale=0.2, bias=-0.4)
+    copy(c_j, c_h, bias=15.0)
+    BC, PM, FO, BO = 0, 30, 90, 92
+    iota(("lf", 0, 16), [[16, 2], [32, 4], [0, 2]], 0)
+    copy(("upo", 0, 16), ("lf", 0, 16))
+    iota(("lf", 16, 46), [[16, K], [0, 2]], 15)
+    copy(("off", BC, BC + 30), ("lf", 16, 46))
+    iota(("lf", 46, 106), [[64, K], [4, 4]], 0)
+    copy(("off", PM, PM + 60), ("lf", 46, 106), bias=c_pm)
+    copy(("off", FO, FO + 1), c_j)
+    copy(("off", BO, BO + 1), col(4))
+    iota(("io40", 0, 40), [[1, 40]], 0)
+    ts(("wpen", 0, 40), ("io40", 0, 40), c_r, ALU.add, E + 15.0, ALU.is_equal)
+    iota(("kt", 0, 16 * K), [[16, K], [-1, 16]], 15)
+    fill(("rst", 0, 16 * K), 0.0)
+    fill(("rst", 0, 16 * K, 16), 1e29)
+    for t in range(R):
+        w = CUT[t] // 64
+        iota(("klf", 10 * t, 10 * t + 2 * w), [[-5, 2], [16, w]], 5)
+        iota(("klf", 10 * t + 2 * w, 10 * t + 10), [[-5, 2], [16, 5 - w]], 16 * w + 5)
+        iota(("ut%d" % t, 0, 32 * w), [[0, 2], [4, 16 * w]], 0)
+        iota(("ut%d" % t, 32 * w, C // 2), [[0, 2], [4, 80 - 16 * w]], 64 * w)
+        copy(("ut%d" % t, 0, C // 2), ("ut%d" % t, 0, C // 2), bias=c_r4)
+    copy(("klf", 0, 20), ("klf", 0, 20), scale=0.2, bias=c_kl)
+    copy(("kli", 0, 20), ("klf", 0, 20))
+    copy(("kl", 0, 20), ("kli", 0, 20))
+    iota(("t20", 0, 48), [[0, 2], [-E, 24]], E)
+    fill(("ones", 0, 516), 1.0)
+    select(("ef", 0, 516), ("ones", 0, 516), [[-1, 516]], ALU.is_equal, 0.0, 3, 4)
+    for b in range(4):
+        quant(("eq", "ep"), 128 * b, 128 * b + 128, ("ef", 3 - b, 515 - b))
+    quant(("uq", "up"), 0, 128, ("uin", 0, 512))
+    add("V", ("pick", 256), [("uq", 0, 128), ("upo", 0, 16)], [("urq", 0, 256)],
+        lambda e: g.vector.tensor_copy(T.urq[:, 0:256].bitcast(dt.uint32),
+                                       T.uq[:, 0:128].bitcast(dt.uint32).indirect(T.upo[:, 0:16])))
+    add("S", ("pick", 256), [("up", 0, 128), ("upo", 0, 16)], [("urp", 0, 256)],
+        lambda e: g.scalar.activation(T.urp[:, 0:256], T.up[:, 0:128].indirect(T.upo[:, 0:16]), ACT.Copy))
+    quant(("nq", "npl"), 0, 128, ("vin", 0, 512))
+    copy(("stf", 0, 2), ("sti", 0, 2))
+    for t in range(R):
+        copy(("bb", 32 * t, 32 * t + 32), ("io40", 0, 32), scale=0.0, bias=("stf", t, t + 1))
+    turn(("bt", 0, 64), ("bb", 0, 64))
+    iota(("lb", 0, 4), [[10, 2], [L, 2]], E + 15)
+    iota(("lb", 4, 8), [[5, 4]], 0)
+    copy(("lb", 0, 4), ("lb", 0, 4), bias=c_tl)
+    copy(("lb", 4, 8), ("lb", 4, 8), bias=c_cl)
+    fill(("bs", 0, 48), 0.0)
+    fill(("jf", 0, 48), 0.0)
+    fill(("pm", 0, 512, 256), 0.0)
+    for t in range(R):
+        copy(("bs", 24 * t + 1, 24 * t + 17), ("bt", 32 * t, 32 * t + 32), ind=("off", BO, BO + 1))
+    copy(("bs", 0, 48, 24), ("bs", 1, 48, 24), bias=-float(E))
+    tt(("bd", 0, 48), ("bs", 0, 48), ("t20", 0, 48), ALU.add)
+    tt(("db", 0, 40), ("bs", 2, 42), ("bs", 1, 41), ALU.subtract)
+    ts(("db", 0, 40), ("db", 0, 40), c_r, ALU.add, E + 16.0, ALU.min)
+    copy(("po", 0, 40), ("db", 0, 40))
+    for t in range(R):
+        s = str(t)
+        for e in range(4):
+            copy(("tf" + s, e, 4 * K, 4), ("bt", 32 * t + 16 * (e % 2), 32 * t + 16 * (e % 2) + K), bias=("lb", e, e + 1))
+            copy(("tf" + s, 4 * K + e, 8 * K, 4), ("bs", 24 * t + 2, 24 * t + 17), bias=("lb", 4 + e, 5 + e))
+        copy(("tl" + s, 0, 8 * K), ("tf" + s, 0, 8 * K))
+        if t == 0:
+            fill(("pen" + s, 0, 64 * K), 0.0)
+            fill(("pen" + s, 0, 64 * K, 4), -1e29)
+        else:
+            iota(("pen" + s, 0, 64 * K), [[0, 64 * K]], 0)
+            select(("pen" + s, 0, 64 * K), ("pen" + s, 0, 64 * K), [[0, 16 * K], [1, 4]], ALU.is_gt, -1e29, 0, 0)
+        copy(("pen" + s, 3, 64 * K, 4), ("wpen", 0, 40), ind=("po", 24 * t, 24 * t + K), scale=1e28)
+        tt(("lc" + s, 0, C // 2), ("bd", 24 * t, 24 * t + 24), ("ut" + s, 0, C // 2), ALU.add,
+           ind=("kl", 10 * t, 10 * t + 10))
+
+    def window(t):
+        s = str(t)
+        head = HEAD if t == 0 else 0
+        if head:
+            send(1, ("wp", 0, head), ("lp0", 0, head), "lay0")
+        send(1, ("vq" + s, 0, B), ("vq" + s, C, L), "win" + s)
+        send(1, ("vp" + s, 0, B), ("vp" + s, C, L), "win" + s)
+        arrival(1, [("vq" + s, C, L), ("vp" + s, C, L)], "win" + s)
+        send(1 + t, ("wp", head, 512), ("lp" + s, head, 512), "lay" + s)
+        send(1 + t, ("wq", 0, 512), ("lq" + s, 0, 512), "lay" + s)
+        arrival(1 + t, [("lq" + s, 0, 512), ("lp" + s, head, 512)] + ([("lp0", 0, head)] if head else []), "lay" + s)
+
+    quant(("vq0", "vp0"), 0, 128, ("xin", 0, a0))
+    window(0)
+    quant(("vq0", "vp0"), 128, C, ("xin", a0, 4 * C))
+    EB = ("eq", "ep")
+
+    def unpack(t, piece, bank):
+        a, b, keep = PIECE[t][piece]
+        V = ("vq%d" % t, "vp%d" % t)
+        for h in range(2):
+            ps = 2 * piece + h
+            mm(ps, ("urq", "urp"), V, a, b, 128 * h)
+            copy(("sc%d" % t, L * h + keep, L * h + b), ("ps%d" % ps, keep - a, b - a))
+        for bb in range(4):
+            ps = bank + (bb + 2) % 4
+            mm(ps, EB, V, a, b, 128 * bb)
+            copy(("dv%d" % t, 4 * keep + bb, 4 * b, 4), ("ps%d" % ps, keep - a, b - a), scale=0.5)
+
+    unpack(0, 0, 4)
+    for t in range(R):
+        s, s2 = str(t), str(t + 1)
+        Z, H, X = ("zq" + s, "zp" + s), ("hq" + s, "hp" + s), ("vq" + s2, "vp" + s2)
+        unpack(t, 1, 4)
+        win = ("sc" + s, 0, 2 * L)
+        for a, b in zip(FINE[t], FINE[t][1:]):
+            tp, tb, dd, aa, s1, pen = [(n + s, 64 * a, 64 * b) for n in ("tp", "tb", "dd", "aa", "s1", "pen")]
+            copy(tp, win, ind=("tl" + s, 4 * a, 4 * b))
+            turn(tb, tp)
+            tt(dd, win, tb, ALU.subtract, ind=("tl" + s, 4 * K + 4 * a, 4 * K + 4 * b))
+            absol(aa, dd, ("off", PM, PM + 4 * (b - a)))
+            scan(s1, pen, aa, ALU.add, ALU.max)
+        for a, b in zip(COARSE[t], COARSE[t][1:]):
+            dist, pm = ("s1" + s, 64 * a + 3, 64 * b, 4), 256 * t
+            scan(("pm", pm + 16 * a + 1, pm + 16 * b + 1), ("rst", 16 * a, 16 * b), dist, ALU.max, ALU.min)
+            tt(("nr" + s, 16 * a, 16 * b), dist, ("pm", pm + 16 * a, pm + 16 * b), ALU.is_ge)
+            scan(("s3" + s, 16 * a, 16 * b), ("nr" + s, 16 * a, 16 * b), ("kt", 16 * a, 16 * b), ALU.mult, ALU.max)
+            copy(("bc" + s, 32 * a, 32 * b), ("s3" + s, 16 * a, 16 * b), ind=("off", BC, BC + 2 * (b - a)))
+            turn(("rr" + s, 32 * a, 32 * b), ("bc" + s, 32 * a, 32 * b))
+        for k in range(K):
+            ts(("ch" + s, 16 * k, 16 * k + 16), ("rr" + s, 32 * k, 32 * k + 32), c_h, ALU.add, -16.0 * k, ALU.add,
+               ind=("off", FO, FO + 1) if k == 0 else ("ch" + s, 16 * k - 16, 16 * k - 15))
+        for i, (a, b) in enumerate(((0, CUT[t]), (CUT[t], C))):
+            ka, kb = (0, (b - 1) // E) if i == 0 else ((a - 1) // E, K)
+            n, la, lb = b - a, a // 2, b // 2
+            copy(("jf", 24 * t + ka + 2, 24 * t + kb + 2), ("ch" + s, 16 * ka, 16 * kb, 16), scale=-1.0, bias=c_j)
+            tt(("l2" + s, la, lb), ("jf", 24 * t, 24 * t + kb + 2), ("lc" + s, la, lb), ALU.add,
+               ind=("kl", 10 * t + la // 16, 10 * t + lb // 16))
+            copy(("li" + s, la, lb), ("l2" + s, la, lb), scale=4.0)
+            dw = ("dv" + s, 0, 4 * L)
+            for c, d in zip(PICKS[t], PICKS[t][1:]):
+                if a <= c < b:
+                    o = la + (c - a) // 4
+                    copy(("zn" + s, 4 * c, 4 * d), dw, ind=("li" + s, o + n // 4, o + n // 4 + (d - c) // 4))
+                    tt(("zt" + s, 4 * c, 4 * d), dw, ("zn" + s, 4 * c, 4 * d), ALU.add, ind=("li" + s, o, o + (d - c) // 4))
+            quant(Z, a, b, ("zt" + s, 4 * a, 4 * b))
+            for bb in range(4):
+                mm(bb, ("lq" + s, "lp" + s), Z, a, b, 128 * bb)
+            for bb in range(4):
+                mm(4 + bb, EB, Z, a, b, 128 * bb, True, False)
+            for bb in range(4):
+                copy(("ht" + s, 4 * a + bb, 4 * b, 4), ("ps%d" % bb, 0, n), scale=0.03125)
+            quant(H, a, b, ("ht" + s, 4 * a, 4 * b))
+            for bb in range(4):
+                mm(4 + bb, EB, H, a, b, 128 * bb, False, True)
+            for bb in range(4):
+                copy(("xt" + s, 4 * a + bb, 4 * b, 4), ("ps%d" % (4 + bb), 0, n))
+            quant(X, a, b, ("xt" + s, 4 * a, 4 * b))
+            if t + 1 == R:
+                dma(T.oc[:, 4 * a:4 * b], u8(("vq2", a, b)), [("vq2", a, b)], [], 4 * n)
+            elif i == 0:
+                window(t + 1)
+                unpack(t + 1, 0, 0)
+        tt(("pout", 16 * t, 16 * t + 16), ("jf", 24 * t + 1, 24 * t + 17), ("bs", 24 * t + 1, 24 * t + 17), ALU.add)
+    dma(T.ol[:], T.pout[0:128:16, 0:32], [("pout", 0, 32)], [], 8)
+    for i, (a, b) in enumerate(((0, CUT[-1]), (CUT[-1], C))):
+        mm(i, ("nq", "npl"), ("vq2", "vp2"), a, b)
+        copy(("ysb", a, b), ("ps%d" % i, 0, b - a))
+        dma(T.y[:, a:b], T.ysb[:, a:b], [("ysb", a, b)], [], 4 * (b - a))
+    for k in range(4):
+        dma(T.osc[4 * k:4 * k + 4, 0:C], T.vp2[32 * k:32 * k + 4, 0:C], [("vp2", 0, C)], [], 10)
+    return ops
+
+
+def depend(ops):
+    seen = {}
+    for i, o in enumerate(ops):
+        deps = {}
+        for wr, rs in ((False, o["reads"]), (True, o["writes"])):
+            for r in rs:
+                bank = SCRATCH[r[0]][0] == "psum"
+                cols = None if bank else set(range(*r[1:]))
+                for j, w, c in seen.get(r[0], []):
+                    if j != i and (bank or ((wr or w) and not cols.isdisjoint(c))):
+                        deps[j] = not (bank and o.get("acc"))
+                if bank:
+                    seen[r[0]] = []
+                seen.setdefault(r[0], []).append((i, wr, cols))
+        for j in o["after"]:
+            deps.setdefault(j, False)
+        o["deps"] = deps
+
+
+def rank_program(g, core, T, topo):
+    if T.rank_of(core) is None:
+        return
+    ops = build(g, T, topo, core)
+    depend(ops)
+    queue = {"V": g.vector, "S": g.scalar, "P": g.tensor, "G": g, "Y": g.sync}
+    known = {e: {} for e in queue}
+    count, waited = {}, {}
+    plan = [(w[0], int(w[1:])) for w in ORDER.split()] or [(o["on"][0], i) for i, o in enumerate(ops)]
+    for at, (e, i) in enumerate(plan):
+        o = ops[i]
+        o["at"] = at
+        if o["kind"] == "arrive":
+            o["mark"], o["clock"] = (o["sem"], o["inc"]), {o["sem"]: o["inc"]}
+            count[o["sem"]] = o["inc"]
+            continue
+        for d in sorted([ops[j] for j, hard in o["deps"].items() if hard], key=lambda d: -d["at"]):
+            sem, n = d["mark"]
+            if known[e].get(sem, 0) < n:
+                queue[e].wait_ge(T.sem[sem], n)
+                waited[sem] = max(waited.get(sem, 0), n)
+                for k, v in d["clock"].items():
+                    known[e][k] = max(known[e].get(k, 0), v)
+        ins = o["emit"](e)
+        if o["kind"] == "send":
+            count["sent"] = count.get("sent", 0) + o["inc"]
+            continue
+        sem, inc = (o["sem"], 16) if o["kind"] == "dma" else ("c" + e, 1)
+        ins.then_inc(T.sem[sem], inc)
+        count[sem] = count.get(sem, 0) + inc
+        o["mark"], o["clock"] = (sem, count[sem]), dict(known[e])
+        o["clock"][sem] = count[sem]
+    for sem, n in count.items():
+        if waited.get(sem, 0) < n:
+            g.wait_ge(T.sem[sem], n)

@@ -4,12 +4,12 @@ C, E, B, R = 320, 20, 112, 2
 L = C + B
 K = 15
 CUT = (128, 192)
-FINE = ((0, 2, 6, 11, 15), (0, 2, 5, 9, 12, 15))
-COARSE = ((0, 6, 11, 15), (0, 5, 9, 15))
-PICKS = ((0, 32, 80, 128, 192, 256, 320), (0, 48, 96, 144, 192, 256, 320))
+FINE = ((0, 3, 6, 11, 15), (0, 3, 7, 10, 15))
+COARSE = ((0, 6, 15), (0, 10, 15))
+PICKS = ((0, 64, 128, 224, 320), (0, 96, 192, 320))
 PIECE = (((0, C, 0), (L - 128, L, C)), ((0, CUT[0], 0), (CUT[0], L, CUT[0])))
 HEAD = 128
-ORDER = "G8 V9 V13 V10 V11 V12 V14 V85 V18 Y1 Y0 Y2 Y3 V86 G29 V48 S17 G21 Y4 S16 V22 V30 G62 Y5 V28 G63 G103 V68 V102 G104 S6 V19 V58 S65 V66 S59 V32 V60 V33 V61 S20 G105 Y7 V15 V64 G49 G25 G23 G31 G107 G108 G34 G35 G39 V69 V54 S56 S83 V27 V55 S70 V110 P111 V67 S81 S78 S93 S94 S91 V71 S77 V73 V89 V53 V79 S80 S76 S112 V50 P113 S114 V90 V26 S95 V74 V75 S87 G40 G47 V52 V51 P115 V116 V96 V82 G36 P117 V84 V24 S118 V92 V97 A106 G37 G41 G42 P125 V57 P123 S126 P119 V124 S135 P121 P129 S150 S145 S44 G98 V140 V136 V141 V72 V142 S143 V137 V151 A109 S138 V146 S120 V144 V139 V155 V45 S130 V156 P127 V157 S158 V147 V159 V170 V46 V171 S148 S122 V152 V172 V149 V173 V160 V174 S128 V161 V175 S38 S153 V88 P133 V185 V162 P131 V186 S132 V187 V154 S134 G99 S163 S190 V164 V165 V176 V166 V177 S192 S188 V167 V191 V193 V189 S43 V178 V194 V179 S168 P197 P195 P196 V169 V180 V181 P198 P201 V182 S205 P202 V183 P200 S203 S204 V184 P199 V206 V235 V207 P210 P209 V236 P208 S214 V237 V212 S242 P211 V213 V215 V216 V243 S240 V241 P229 G217 P223 P227 P225 S238 S226 S228 V239 G218 V244 S224 P231 P233 S230 S232 S234 P247 P248 P245 V100 V267 V256 S255 P246 S253 V254 P249 P252 P251 V257 P250 P258 P261 V265 S262 P259 P260 V264 S263 V266 V101 A219 P270 P268 V269 S271 V290 V291 P272 S285 S280 V286 G220 S295 V281 G221 V287 V282 S273 S288 S283 P274 V292 S300 P278 V289 V284 V296 V305 S293 V306 V301 V307 V297 V302 V294 S308 S298 V309 V310 S303 V299 V311 V320 V304 P276 S277 V312 V315 V321 V316 S313 V322 V317 S318 V323 V314 V324 V325 V326 V327 V319 V328 V329 S279 V335 V330 V336 V331 V337 V332 V333 V334 V370 S275 S340 S338 S342 V371 V341 S344 V372 V339 V343 S375 V345 S373 V346 V376 V374 V377 V401 A222 P349 P348 P347 P352 P350 P354 P351 S357 S356 S355 S358 P353 P380 P379 P378 P381 S402 V359 S388 P361 V387 P363 S386 S389 S367 V365 P360 V390 P362 V366 P383 P392 P385 S364 V368 P382 P384 S369 P393 S397 P403 P394 V396 S398 V404 P391 V395 S405 V399 P406 S400 Y412 S409 Y410 V407 S408 Y411"
+ORDER = "G8 V48 V12 V13 V9 V10 V11 V111 V14 S1 V67 V15 V68 V28 G29 V30 G116 V66 S16 G21 Y0 Y2 Y3 G62 G63 S20 V22 V85 S65 V58 Y4 S5 S60 S59 V19 V86 S64 G114 V102 S115 V61 S78 G103 G104 G105 Y6 V54 V18 V32 V55 S69 S56 S89 G49 V83 V110 V112 S17 S70 G25 A106 S91 G23 G31 G107 P118 P120 G108 S81 S79 V27 V71 V33 S77 S82 V73 S92 S90 S119 V80 V53 V74 Y7 V52 V76 S95 P128 G34 S121 V75 S94 V24 V51 S87 A109 G35 G39 P130 S131 V50 V84 V96 V113 G40 G47 G36 S129 P132 V26 V133 P126 V147 V148 P124 S142 P140 S152 S157 S44 V143 S125 V149 V144 S145 V153 V158 V154 P122 S150 S93 V146 V151 S123 V45 V162 S155 P134 V159 P136 V163 V46 S160 V164 S165 S135 G37 G41 G42 S38 S137 V156 V167 V161 V168 V166 S169 G98 V170 V178 S127 V171 V179 V172 V180 V72 S173 P138 V175 S139 V181 V88 S43 S141 V187 V176 V174 V188 V117 V189 S177 G99 V57 V182 V97 V183 S192 V193 S190 V191 V184 S100 V194 V185 P196 S204 P198 V186 P197 S205 P195 S203 V235 V206 P201 V236 P199 P200 V237 P202 V207 P210 P209 P211 S238 V265 S213 V101 V214 V215 V239 P208 S212 V216 P223 G217 G218 A219 S240 P225 V241 V242 S224 P227 P229 S226 P231 S228 P233 S232 P245 S234 P243 P244 S230 S251 P246 P250 S252 P248 P247 P249 V253 V254 V255 P259 P258 V263 S262 P256 S260 P257 V261 V264 P268 P266 P272 P276 G220 G221 P274 S269 V267 V288 S283 V289 S278 V284 S293 V290 V279 S291 V285 S286 V280 V294 V292 V287 S281 S275 S277 A222 V282 V295 V298 V299 V300 S296 V297 V303 V306 V304 S301 V302 V307 S305 V314 V308 S309 V315 V311 S273 V316 V312 V317 V310 V318 V319 S313 P270 V323 V320 V324 S271 V321 V325 V322 S326 S328 V354 V355 V356 V383 V327 V329 V330 S357 P334 P333 P331 P332 S342 S341 V358 P338 S339 V340 V359 P335 P337 P336 P360 P362 V343 P344 P345 V368 P346 S350 V348 P347 V349 V351 P361 P363 S370 S371 V369 V352 V372 P364 P366 P365 P367 S353 P385 P375 S379 P373 P374 Y384 V386 P376 S378 V377 V380 S387 V381 S391 Y382 S392 P388 V389 Y393 S394 Y390"
 Q4, U8, F32, BF, I32, U16 = "float8_e4m3fn_x4", "uint8", "float32", "bfloat16", "int32", "uint16"
 
 SCRATCH = {}
@@ -21,7 +21,8 @@ for _n, _w, _d in (("xin", 4 * C, BF), ("uin", 512, BF), ("vin", 512, BF), ("sti
                    ("kli", 20, I32), ("klf", 20, F32), ("kl", 20, U16), ("kt", 16 * K, BF), ("rst", 16 * K, F32),
                    ("stf", 2, F32), ("bb", 64, F32), ("bt", 64, F32), ("lb", 8, F32), ("bs", 48, F32),
                    ("bd", 48, F32), ("db", 40, F32), ("po", 40, U16), ("jf", 48, F32), ("pm", 512, F32),
-                   ("pout", 32, F32), ("ysb", C, F32), ("vq2", C, Q4), ("vp2", C, U8)):
+                   ("pout", 32, F32), ("tab", 16, F32), ("par", 48, F32), ("nf", 32, F32), ("nn", 32, U16),
+                   ("ysb", C, F32), ("vq2", C, Q4), ("vp2", C, U8)):
     SCRATCH[_n] = ("sbuf", [128, _w], _d)
 for _t in range(R):
     for _n, _w, _d in (("vq", L, Q4), ("vp", L, U8), ("lq", 512, Q4), ("lp", 512, U8), ("sc", 2 * L, F32),
@@ -29,8 +30,9 @@ for _t in range(R):
                        ("ut", C // 2, F32), ("lc", C // 2, F32), ("l2", C // 2, F32), ("li", C // 2, U16),
                        ("tp", 64 * K, F32), ("tb", 64 * K, F32), ("dd", 64 * K, F32), ("aa", 64 * K, F32),
                        ("s1", 64 * K, F32), ("nr", 16 * K, BF), ("s3", 16 * K, BF), ("bc", 32 * K, BF),
-                       ("rr", 32 * K, BF), ("ch", 16 * K, U16), ("zn", 4 * C, F32), ("zt", 4 * C, BF), ("zq", C, Q4),
-                       ("zp", C, U8), ("ht", 4 * C, BF), ("hq", C, Q4), ("hp", C, U8), ("xt", 4 * C, BF)):
+                       ("rr", 32 * K, BF), ("ch", 16 * K + 18, U16), ("g2", 16 * K, BF), ("zn", 4 * C, F32),
+                       ("zt", 4 * C, BF), ("zq", C, Q4), ("zp", C, U8), ("ht", 4 * C, BF), ("hq", C, Q4),
+                       ("hp", C, U8), ("xt", 4 * C, BF)):
         SCRATCH["%s%d" % (_n, _t)] = ("sbuf", [128, _w], _d)
 for _b in range(8):
     SCRATCH["ps%d" % _b] = ("psum", [128, 512], F32)
@@ -153,9 +155,9 @@ def build(g, T, topo, core):
                                                 T.sem.sent, pid, rid, topo.mask(core, dst)),
                          kind="send", inc=len(topo.engines(core, dst)), after=sends[-1:]))
 
-    def arrival(step, lands, sem):
+    def arrival(step, lands, sem, calls):
         add("A", ("arrive", 0), [], lands, None, kind="arrive", sem=sem, after=sends[-1:],
-            inc=len(lands) * len(topo.engines(cores[(rank + step) % n_r], core)))
+            inc=calls * len(topo.engines(cores[(rank + step) % n_r], core)))
 
     a0 = 4 * 128
     dma(T.xin[:, 0:a0], T.x[:, 0:a0], [], [("xin", 0, a0)], 2 * a0)
@@ -182,7 +184,7 @@ def build(g, T, topo, core):
     copy(c_r4, c_r, scale=0.25)
     copy(c_kl, c_r, scale=0.2, bias=-0.4)
     copy(c_j, c_h, bias=15.0)
-    BC, PM, FO, BO = 0, 30, 90, 92
+    BC, PM, FO, BO, F2 = 0, 30, 90, 92, 94
     iota(("lf", 0, 16), [[16, 2], [32, 4], [0, 2]], 0)
     copy(("upo", 0, 16), ("lf", 0, 16))
     iota(("lf", 16, 46), [[16, K], [0, 2]], 15)
@@ -206,7 +208,7 @@ def build(g, T, topo, core):
     copy(("klf", 0, 20), ("klf", 0, 20), scale=0.2, bias=c_kl)
     copy(("kli", 0, 20), ("klf", 0, 20))
     copy(("kl", 0, 20), ("kli", 0, 20))
-    iota(("t20", 0, 48), [[0, 2], [-E, 24]], E)
+    iota(("t20", 0, 48), [[0, 2], [-2 * E, 12], [16 - E, 2]], E)
     fill(("ones", 0, 516), 1.0)
     select(("ef", 0, 516), ("ones", 0, 516), [[-1, 516]], ALU.is_equal, 0.0, 3, 4)
     for b in range(4):
@@ -259,14 +261,21 @@ def build(g, T, topo, core):
             send(1, ("wp", 0, head), ("lp0", 0, head), "lay0")
         send(1, ("vq" + s, 0, B), ("vq" + s, C, L), "win" + s)
         send(1, ("vp" + s, 0, B), ("vp" + s, C, L), "win" + s)
-        arrival(1, [("vq" + s, C, L), ("vp" + s, C, L)], "win" + s)
+        arrival(1, [("vq" + s, C, L), ("vp" + s, C, L)], "win" + s, 2)
         send(1 + t, ("wp", head, 512), ("lp" + s, head, 512), "lay" + s)
         send(1 + t, ("wq", 0, 512), ("lq" + s, 0, 512), "lay" + s)
-        arrival(1 + t, [("lq" + s, 0, 512), ("lp" + s, head, 512)] + ([("lp0", 0, head)] if head else []), "lay" + s)
+        arrival(1 + t, [("lq" + s, 0, 512), ("lp" + s, 0, 512)], "lay" + s, 3 if head else 2)
 
     quant(("vq0", "vp0"), 0, 128, ("xin", 0, a0))
     window(0)
     quant(("vq0", "vp0"), 128, C, ("xin", a0, 4 * C))
+    fill(("off", F2, F2 + 1), 15)
+    fill(("nn", 0, 32, 16), 0)
+    fill(("jf", 1, 48, 24), -16.0)
+    iota(("tab", 0, 16), [[16, 16]], 32)
+    copy(("tab", 0, 16), ("tab", 0, 16), bias=c_h)
+    iota(("par", 0, 48), [[0, 24], [16, 2]], 0)
+    tt(("par", 0, 48), ("par", 0, 48), ("bs", 0, 48), ALU.add)
     EB = ("eq", "ep")
 
     def unpack(t, piece, bank):
@@ -301,13 +310,21 @@ def build(g, T, topo, core):
             scan(("s3" + s, 16 * a, 16 * b), ("nr" + s, 16 * a, 16 * b), ("kt", 16 * a, 16 * b), ALU.mult, ALU.max)
             copy(("bc" + s, 32 * a, 32 * b), ("s3" + s, 16 * a, 16 * b), ind=("off", BC, BC + 2 * (b - a)))
             turn(("rr" + s, 32 * a, 32 * b), ("bc" + s, 32 * a, 32 * b))
-        for k in range(K):
-            ts(("ch" + s, 16 * k, 16 * k + 16), ("rr" + s, 32 * k, 32 * k + 32), c_h, ALU.add, -16.0 * k, ALU.add,
-               ind=("off", FO, FO + 1) if k == 0 else ("ch" + s, 16 * k - 16, 16 * k - 15))
+            nf, nn = ("nf", 16 * t + a + 1, 16 * t + b + 1), ("nn", 16 * t + a + 1, 16 * t + b + 1)
+            tt(nf, ("s3" + s, 16 * a + 15, 16 * b, 16), ("tab", a, b), ALU.add)
+            copy(nn, nf)
+            copy(("g2" + s, 16 * a, 16 * b), ("rr" + s, 0, 32 * b), ind=("nn", 16 * t + a, 16 * t + b))
+        ch, g2 = "ch" + s, "g2" + s
+        ts((ch, 1, 17), ("rr" + s, 0, 32), 0.0, ALU.add, ind=("off", FO, FO + 1))
+        ts((ch, 17, 33), (g2, 16, 32), 0.0, ALU.add, ind=("off", F2, F2 + 1))
+        for k in range(1, K, 2):
+            w = min(2, K - 1 - k)
+            ts((ch, 16 * k + 17, 16 * (k + w) + 17), (g2, 16 * k + 16, 16 * (k + w) + 16), -16.0 * (k + 1), ALU.add,
+               ind=(ch, 16 * k, 16 * k + w))
         for i, (a, b) in enumerate(((0, CUT[t]), (CUT[t], C))):
             ka, kb = (0, (b - 1) // E) if i == 0 else ((a - 1) // E, K)
             n, la, lb = b - a, a // 2, b // 2
-            copy(("jf", 24 * t + ka + 2, 24 * t + kb + 2), ("ch" + s, 16 * ka, 16 * kb, 16), scale=-1.0, bias=c_j)
+            copy(("jf", 24 * t + ka + 2, 24 * t + kb + 2), (ch, 16 * ka + 16, 16 * kb + 16, 16), scale=-1.0, bias=15.0)
             tt(("l2" + s, la, lb), ("jf", 24 * t, 24 * t + kb + 2), ("lc" + s, la, lb), ALU.add,
                ind=("kl", 10 * t + la // 16, 10 * t + lb // 16))
             copy(("li" + s, la, lb), ("l2" + s, la, lb), scale=4.0)
@@ -335,7 +352,7 @@ def build(g, T, topo, core):
             elif i == 0:
                 window(t + 1)
                 unpack(t + 1, 0, 0)
-        tt(("pout", 16 * t, 16 * t + 16), ("jf", 24 * t + 1, 24 * t + 17), ("bs", 24 * t + 1, 24 * t + 17), ALU.add)
+        tt(("pout", 16 * t, 16 * t + 16), ("jf", 24 * t + 1, 24 * t + 17), ("par", 24 * t + 1, 24 * t + 17), ALU.add)
     dma(T.ol[:], T.pout[0:128:16, 0:32], [("pout", 0, 32)], [], 8)
     for i, (a, b) in enumerate(((0, CUT[-1]), (CUT[-1], C))):
         mm(i, ("nq", "npl"), ("vq2", "vp2"), a, b)

@@ -3,65 +3,71 @@ from concourse.mybir import dt, AluOpType, ActivationFunctionType
 C, E, B, R = 320, 20, 112, 2
 L = C + B
 K = 15
-CUT = (128, 192)
-FINE = ((0, 3, 6, 11, 15), (0, 3, 7, 10, 15))
-COARSE = ((0, 6, 15), (0, 10, 15))
-PICKS = ((0, 64, 128, 224, 320), (0, 96, 192, 320))
-PIECE = (((0, C, 0), (L - 128, L, C)), ((0, CUT[0], 0), (CUT[0], L, CUT[0])))
+CHUNK = ((0, 6), (6, 12), (12, 15))
+SUB = ((3, 4, 1), (2, 2, 2))
+PIECE = (((0, 0, 132), (132, 132, 260), (192, 260, C)), ((0, 0, 188), (188, 188, C)))
+ZN = ((0, 24, 40, 58, 80), (0, 10, 34, 48, 70, 80))
+ZT = ((-1, 19, 33, 49, 65, 80), (-1, 5, 33, 47, 65, 80))
+LI = ((0, 10, 25, 40, 70, 85), (0, 10, 40, 55, 70, 85))
+AHEAD = 1.2
 HEAD = 128
-ORDER = "G8 V48 V12 V13 V9 V10 V11 V111 V14 S1 V67 V15 V68 V28 G29 V30 G116 V66 S16 G21 Y0 Y2 Y3 G62 G63 S20 V22 V85 S65 V58 Y4 S5 S60 S59 V19 V86 S64 G114 V102 S115 V61 S78 G103 G104 G105 Y6 V54 V18 V32 V55 S69 S56 S89 G49 V83 V110 V112 S17 S70 G25 A106 S91 G23 G31 G107 P118 P120 G108 S81 S79 V27 V71 V33 S77 S82 V73 S92 S90 S119 V80 V53 V74 Y7 V52 V76 S95 P128 G34 S121 V75 S94 V24 V51 S87 A109 G35 G39 P130 S131 V50 V84 V96 V113 G40 G47 G36 S129 P132 V26 V133 P126 V147 V148 P124 S142 P140 S152 S157 S44 V143 S125 V149 V144 S145 V153 V158 V154 P122 S150 S93 V146 V151 S123 V45 V162 S155 P134 V159 P136 V163 V46 S160 V164 S165 S135 G37 G41 G42 S38 S137 V156 V167 V161 V168 V166 S169 G98 V170 V178 S127 V171 V179 V172 V180 V72 S173 P138 V175 S139 V181 V88 S43 S141 V187 V176 V174 V188 V117 V189 S177 G99 V57 V182 V97 V183 S192 V193 S190 V191 V184 S100 V194 V185 P196 S204 P198 V186 P197 S205 P195 S203 V235 V206 P201 V236 P199 P200 V237 P202 V207 P210 P209 P211 S238 V265 S213 V101 V214 V215 V239 P208 S212 V216 P223 G217 G218 A219 S240 P225 V241 V242 S224 P227 P229 S226 P231 S228 P233 S232 P245 S234 P243 P244 S230 S251 P246 P250 S252 P248 P247 P249 V253 V254 V255 P259 P258 V263 S262 P256 S260 P257 V261 V264 P268 P266 P272 P276 G220 G221 P274 S269 V267 V288 S283 V289 S278 V284 S293 V290 V279 S291 V285 S286 V280 V294 V292 V287 S281 S275 S277 A222 V282 V295 V298 V299 V300 S296 V297 V303 V306 V304 S301 V302 V307 S305 V314 V308 S309 V315 V311 S273 V316 V312 V317 V310 V318 V319 S313 P270 V323 V320 V324 S271 V321 V325 V322 S326 S328 V354 V355 V356 V383 V327 V329 V330 S357 P334 P333 P331 P332 S342 S341 V358 P338 S339 V340 V359 P335 P337 P336 P360 P362 V343 P344 P345 V368 P346 S350 V348 P347 V349 V351 P361 P363 S370 S371 V369 V352 V372 P364 P366 P365 P367 S353 P385 P375 S379 P373 P374 Y384 V386 P376 S378 V377 V380 S387 V381 S391 Y382 S392 P388 V389 Y393 S394 Y390"
+PAD = 4 * E
+TG2, TRR, TW = 32, 192, 384
 Q4, U8, F32, BF, I32, U16 = "float8_e4m3fn_x4", "uint8", "float32", "bfloat16", "int32", "uint16"
 
 SCRATCH = {}
 for _n, _w, _d in (("xin", 4 * C, BF), ("uin", 512, BF), ("vin", 512, BF), ("sti", 2, I32), ("wq", 512, Q4),
                    ("wp", 512, U8), ("uq", 128, Q4), ("up", 128, U8), ("urq", 256, Q4), ("urp", 256, U8),
                    ("nq", 128, Q4), ("npl", 128, U8), ("ones", 516, BF), ("ef", 516, BF), ("eq", 512, Q4),
-                   ("ep", 512, U8), ("pi", 2, I32), ("ai", 8, I32), ("af", 16, F32), ("io40", 40, F32),
-                   ("wpen", 40, F32), ("t20", 48, F32), ("lf", 112, F32), ("upo", 16, U16), ("off", 96, U16),
-                   ("kli", 20, I32), ("klf", 20, F32), ("kl", 20, U16), ("kt", 16 * K, BF), ("rst", 16 * K, F32),
-                   ("stf", 2, F32), ("bb", 64, F32), ("bt", 64, F32), ("lb", 8, F32), ("bs", 48, F32),
-                   ("bd", 48, F32), ("db", 40, F32), ("po", 40, U16), ("jf", 48, F32), ("pm", 512, F32),
-                   ("pout", 32, F32), ("tab", 16, F32), ("par", 48, F32), ("nf", 32, F32), ("nn", 32, U16),
-                   ("ysb", C, F32), ("vq2", C, Q4), ("vp2", C, U8)):
+                   ("ep", 512, U8), ("pi", 2, I32), ("ai", 8, I32), ("af", 24, F32), ("io40", 40, F32),
+                   ("wpen", 40, F32), ("lf", 48, F32), ("upo", 16, U16), ("off", 24, U16), ("items", 128, F32),
+                   ("il", 256, F32), ("it", 256, F32), ("lam", 8, U16), ("kli", 6, I32), ("klf", 6, F32),
+                   ("kl", 6, U16), ("kt", 192, BF), ("rst", 96, F32), ("rs2", 192, BF), ("stf", 2, F32),
+                   ("bb", 64, F32), ("bt", 256, F32), ("bs", 32, F32), ("db", 32, F32), ("po", 32, U16),
+                   ("bc0", 90, F32), ("cc", 8, F32), ("nn", 32, U16),
+                   ("tp", 64 * K, F32), ("tb", 64 * K, F32), ("dd", 64 * K, F32), ("aa", 64 * K, F32),
+                   ("s1", 64 * K, F32), ("pm", 256, F32), ("nr", 32 * K, BF), ("s3", 3 * 224, BF),
+                   ("bc", 32 * K, BF), ("tt", 3 * TW, BF), ("ch", 64, U16), ("zn", 4 * C + 16, F32),
+                   ("pout", 32, F32), ("ysb", C, F32), ("vq2", C, Q4), ("vp2", C, U8)):
     SCRATCH[_n] = ("sbuf", [128, _w], _d)
 for _t in range(R):
-    for _n, _w, _d in (("vq", L, Q4), ("vp", L, U8), ("lq", 512, Q4), ("lp", 512, U8), ("sc", 2 * L, F32),
-                       ("dv", 4 * L, F32), ("tf", 8 * K, F32), ("tl", 8 * K, U16), ("pen", 64 * K, BF),
-                       ("ut", C // 2, F32), ("lc", C // 2, F32), ("l2", C // 2, F32), ("li", C // 2, U16),
-                       ("tp", 64 * K, F32), ("tb", 64 * K, F32), ("dd", 64 * K, F32), ("aa", 64 * K, F32),
-                       ("s1", 64 * K, F32), ("nr", 16 * K, BF), ("s3", 16 * K, BF), ("bc", 32 * K, BF),
-                       ("rr", 32 * K, BF), ("ch", 16 * K + 18, U16), ("g2", 16 * K, BF), ("zn", 4 * C, F32),
-                       ("zt", 4 * C, BF), ("zq", C, Q4), ("zp", C, U8), ("ht", 4 * C, BF), ("hq", C, Q4),
-                       ("hp", C, U8), ("xt", 4 * C, BF)):
+    for _n, _w, _d in (("vq", 512, Q4), ("vp", 512, U8), ("lq", 512, Q4), ("lp", 512, U8), ("sc", 2 * L, F32),
+                       ("dv", PAD + 4 * L, F32), ("tl", 128, U16), ("pen", 64 * K, BF), ("base", 80, F32),
+                       ("wv", 96, F32), ("li", 96, U16), ("zt", 4 * C + 16, BF), ("zq", 388, Q4), ("zp", 388, U8),
+                       ("ht", 4 * C, BF), ("hq", 388, Q4), ("hp", 388, U8), ("xt", 4 * C, BF)):
         SCRATCH["%s%d" % (_n, _t)] = ("sbuf", [128, _w], _d)
 for _b in range(8):
     SCRATCH["ps%d" % _b] = ("psum", [128, 512], F32)
-SEMAPHORES = ["cV", "cS", "cP", "cG", "sent", "win0", "win1", "lay0", "lay1"] + ["d%d" % i for i in range(20)]
+SEMAPHORES = ["cV", "cS", "cP", "cG", "sent", "win0", "win1", "lay0", "lay1"] + ["d%d" % i for i in range(24)]
 
 ALU, ACT = AluOpType, ActivationFunctionType
 
 
 def build(g, T, topo, core):
-    ops = []
+    ops, bank, tag, behind = [], {}, [""], [[]]
     cores, rank = T.cores, T.rank_of(core)
     n_r = len(cores)
     queue = {"S": g.scalar, "Y": g.sync}
 
     def ap(r):
-        return T[r[0]][:, r[1]:r[2]] if len(r) == 3 else T[r[0]][:, r[1]:r[2]:r[3]]
+        t = T["ps%d" % bank[r[0]]] if r[0][0] == "@" else T[r[0]]
+        return t[:, r[1]:r[2]] if len(r) == 3 else t[:, r[1]:r[2]:r[3]]
 
     def cnt(r):
         return len(range(*r[1:]))
 
+    def dtype(r):
+        return F32 if r[0][0] == "@" else SCRATCH[r[0]][2]
+
     def add(on, size, reads, writes, emit, **kw):
         o = dict(on=on, size=size, reads=[x for x in reads if isinstance(x, tuple)], writes=writes, emit=emit,
-                 after=[], kind="op")
+                 after=list(behind[0]), kind="op", mms=[], tag=tag[0])
         o.update(kw)
         ops.append(o)
         return len(ops) - 1
 
     def kind(ind, o, *rs):
-        two = all(SCRATCH[r[0]][2] in (BF, U16) for r in (o,) + rs)
+        two = all(dtype(r) in (BF, U16) for r in (o,) + rs)
         return ("pick" if ind else "half" if two else "one", cnt(o))
 
     def src(i, ind):
@@ -70,8 +76,8 @@ def build(g, T, topo, core):
     def scal(s):
         return ap(s) if isinstance(s, tuple) else s
 
-    def copy(o, i, ind=None, scale=None, bias=None):
-        whole = SCRATCH[o[0]][2] in (U16, I32) or SCRATCH[i[0]][2] in (U16, I32)
+    def copy(o, i, ind=None, scale=None, bias=None, on="SV", **more):
+        whole = dtype(o) in (U16, I32) or dtype(i) in (U16, I32)
 
         def emit(e):
             if e == "S":
@@ -88,10 +94,10 @@ def build(g, T, topo, core):
             if scale is None:
                 return g.vector.tensor_scalar(ap(o), src(i, ind), scal(bias), None, ALU.add)
             return g.vector.tensor_scalar(ap(o), src(i, ind), scal(scale), scal(bias), ALU.mult, ALU.add)
-        return add("V" if whole else "VS", kind(ind, o, i), [i, ind, scale, bias], [o], emit)
+        return add("V" if whole else on, kind(ind, o, i), [i, ind, scale, bias], [o], emit, **more)
 
-    def absol(o, i, ind):
-        return add("S", kind(ind, o, i), [i, ind], [o], lambda e: g.scalar.activation(ap(o), src(i, ind), ACT.Abs))
+    def absol(o, i):
+        return add("S", kind(None, o, i), [i], [o], lambda e: g.scalar.activation(ap(o), ap(i), ACT.Abs))
 
     def ts(o, i, s1, op0, s2=None, op1=None, ind=None):
         def emit(e):
@@ -116,7 +122,7 @@ def build(g, T, topo, core):
 
     def iota(o, pat, base, cm=0):
         def emit(e):
-            if SCRATCH[o[0]][2] == I32:
+            if dtype(o) == I32:
                 return g.iota(ap(o), pat, base, cm)
             return g.iota(ap(o), pat, base, cm, allow_small_or_imprecise_dtypes=True)
         return add("G", ("pool", cnt(o)), [], [o], emit)
@@ -124,15 +130,23 @@ def build(g, T, topo, core):
     def select(o, i, pat, op, other, base, cm):
         return add("G", ("pool", cnt(o)), [i], [o], lambda e: g.affine_select(ap(o), ap(i), pat, op, other, base, cm))
 
-    def quant(q, a, b, i):
+    def quant(q, a, i):
+        b = a + cnt(i) // 4
         c, p = (q[0], a, b), (q[1], a, b)
         return add("V", ("quant", cnt(i)), [i], [c, p], lambda e: g.vector.quantize_mx(ap(c), ap(p), ap(i)))
 
-    def mm(bank, w, x, a, b, wa=0, start=True, stop=True):
-        wq_, wp_, xq_, xp_ = (w[0], wa, wa + 128), (w[1], wa, wa + 128), (x[0], a, b), (x[1], a, b)
-        o = ("ps%d" % bank, 0, b - a)
-        return add("P", ("mm", b - a), [wq_, wp_, xq_, xp_], [o],
-                   lambda e: g.tensor.matmul_mx(ap(o), ap(wq_), ap(wp_), ap(xq_), ap(xp_), start, stop), acc=not start)
+    named = [0]
+
+    def product(o, terms, a, b, keep, scale=None):
+        named[0] += 1
+        ps, mms = ("@%d" % named[0], 0, b - a), []
+        for i, (w, wa, x) in enumerate(terms):
+            r = [(w[0], wa, wa + 128), (w[1], wa, wa + 128), (x[0], a, b), (x[1], a, b)]
+
+            def emit(e, r=r, i=i):
+                return g.tensor.matmul_mx(ap(ps), ap(r[0]), ap(r[1]), ap(r[2]), ap(r[3]), i == 0, i + 1 == len(terms))
+            mms.append(add("P", ("mm", b - a), r, [ps], emit, kind="mm", acc=i > 0))
+        return copy(o, (ps[0], keep, keep + cnt(o)), scale=scale, mms=mms)
 
     ndma = [0]
 
@@ -149,7 +163,7 @@ def build(g, T, topo, core):
     def send(step, s, d, sem):
         dst = cores[(rank - step) % n_r]
         rid, pid, _ = topo.addr(dst)
-        codes = SCRATCH[s[0]][2] == Q4
+        codes = dtype(s) == Q4
         sends.append(add("G", ("send", cnt(s) * (4 if codes else 1)), [s], [],
                          lambda e: g.remote_dma(u8(d) if codes else ap(d), u8(s) if codes else ap(s), T.sem[sem],
                                                 T.sem.sent, pid, rid, topo.mask(core, dst)),
@@ -170,197 +184,203 @@ def build(g, T, topo, core):
     dma(T.vin[:], T.v[:], [], [("vin", 0, 512)], 1024)
 
     iota(("pi", 0, 1), [[0, 1]], 0, 1)
-    for j, m in enumerate((15, 16, 3, None, 31)):
-        if m is None:
-            ts(("ai", j, j + 1), ("pi", 0, 1), 2, ALU.arith_shift_right, 3, ALU.bitwise_and)
-        else:
-            ts(("ai", j, j + 1), ("pi", 0, 1), m, ALU.bitwise_and)
-    copy(("af", 0, 5), ("ai", 0, 5))
+    for j, m in enumerate((15, 16, 1)):
+        ts(("ai", j, j + 1), ("pi", 0, 1), m, ALU.bitwise_and)
+    copy(("af", 0, 3), ("ai", 0, 3))
     col = lambda j: ("af", j, j + 1)
-    c_r, c_h, c_tl, c_cl, c_pm, c_r4, c_kl, c_j = col(0), col(1), col(6), col(7), col(8), col(9), col(10), col(11)
-    ts(c_tl, c_h, 5.0 / 16, ALU.mult, c_r, ALU.subtract)
-    copy(c_cl, c_h, scale=L / 16.0, bias=c_r)
-    copy(c_pm, col(2), scale=16.0, bias=col(3))
-    copy(c_r4, c_r, scale=0.25)
-    copy(c_kl, c_r, scale=0.2, bias=-0.4)
-    copy(c_j, c_h, bias=15.0)
-    BC, PM, FO, BO, F2 = 0, 30, 90, 92, 94
+    c_r, c_h, c_lh, c_tl, c_it, c_kl, c_1, c_2, c_al, c_be, c_x, c_y, c_nn = map(col, [0, 1] + list(range(5, 16)))
+    copy(c_lh, c_h, scale=L / 16.0)
+    copy(c_tl, c_r, scale=-1.0, bias=E + 15.0)
+    copy(c_it, col(2), scale=63.0, bias=c_r)
+    copy(c_kl, c_r, scale=0.2, bias=0.6)
+    ts(c_1, c_r, 5.0, ALU.is_ge)
+    ts(c_2, c_r, 10.0, ALU.is_ge)
+    copy(c_x, c_h, scale=-1.0, bias=float(TG2 - TRR))
+    copy(c_y, c_x, scale=c_1, bias=c_h)
+    copy(c_al, c_2, scale=-float(TG2), bias=c_y)
+    copy(c_be, c_2, scale=-80.0, bias=96.0)
+    copy(c_nn, c_h, bias=32.0)
+    iota(("cc", 0, 4), [[0, 2], [-1, 2]], 1)
+    iota(("cc", 4, 8), [[0, 2], [-96, 2]], TRR - 64)
+    copy(("cc", 0, 4), ("cc", 0, 4), scale=c_be, bias=c_al)
+    tt(("cc", 0, 4), ("cc", 0, 4), ("cc", 4, 8), ALU.add)
+    IL, FO, BO = 0, 16, 18
+    copy(("off", FO, FO + 1), c_al, bias=TRR + 15.0)
+    copy(("off", BO, BO + 1), c_r, bias=c_h)
     iota(("lf", 0, 16), [[16, 2], [32, 4], [0, 2]], 0)
     copy(("upo", 0, 16), ("lf", 0, 16))
-    iota(("lf", 16, 46), [[16, K], [0, 2]], 15)
-    copy(("off", BC, BC + 30), ("lf", 16, 46))
-    iota(("lf", 46, 106), [[64, K], [4, 4]], 0)
-    copy(("off", PM, PM + 60), ("lf", 46, 106), bias=c_pm)
-    copy(("off", FO, FO + 1), c_j)
-    copy(("off", BO, BO + 1), col(4))
+    iota(("items", 0, 48), [[6, 2], [64, 4], [1, 6]], 0)
+    iota(("items", 48, 60), [[64, 4], [1, 3]], 12)
+    fill(("items", 60, 64), 0.0)
+    copy(("items", 64, 128), ("items", 0, 64), bias=16.0)
+    iota(("lf", 16, 24), [[16, 4], [1, 2]], 0)
+    iota(("lf", 24, 32), [[16, 4], [64, 2]], 0)
+    copy(("off", IL, IL + 8), ("lf", 16, 24), bias=c_it)
+    copy(("off", IL + 8, IL + 16), ("lf", 24, 32), bias=c_r)
+    copy(("il", 0, 256), ("items", 0, 128), ind=("off", IL, IL + 16))
+    turn(("it", 0, 256), ("il", 0, 256))
+    copy(("lam", 0, 4), ("it", 0, 128, 32))
+    copy(("lam", 4, 8), ("it", 128, 256, 32), bias=1.0)
     iota(("io40", 0, 40), [[1, 40]], 0)
     ts(("wpen", 0, 40), ("io40", 0, 40), c_r, ALU.add, E + 15.0, ALU.is_equal)
-    iota(("kt", 0, 16 * K), [[16, K], [-1, 16]], 15)
-    fill(("rst", 0, 16 * K), 0.0)
-    fill(("rst", 0, 16 * K, 16), 1e29)
-    for t in range(R):
-        w = CUT[t] // 64
-        iota(("klf", 10 * t, 10 * t + 2 * w), [[-5, 2], [16, w]], 5)
-        iota(("klf", 10 * t + 2 * w, 10 * t + 10), [[-5, 2], [16, 5 - w]], 16 * w + 5)
-        iota(("ut%d" % t, 0, 32 * w), [[0, 2], [4, 16 * w]], 0)
-        iota(("ut%d" % t, 32 * w, C // 2), [[0, 2], [4, 80 - 16 * w]], 64 * w)
-        copy(("ut%d" % t, 0, C // 2), ("ut%d" % t, 0, C // 2), bias=c_r4)
-    copy(("klf", 0, 20), ("klf", 0, 20), scale=0.2, bias=c_kl)
-    copy(("kli", 0, 20), ("klf", 0, 20))
-    copy(("kl", 0, 20), ("kli", 0, 20))
-    iota(("t20", 0, 48), [[0, 2], [-2 * E, 12], [16 - E, 2]], E)
     fill(("ones", 0, 516), 1.0)
+    iota(("kt", 0, 192), [[32, 6], [-1, 16], [-256, 2]], 15)
+    fill(("rst", 0, 96), 0.0)
+    fill(("rst", 0, 96, 16), 1e29)
+    fill(("rs2", 0, 192), 0.0)
+    fill(("rs2", 0, 192, 32), 1e29)
+    for q, (a, b) in enumerate(CHUNK):
+        copy(("nr", 32 * a + 1, 32 * b, 2), ("ones", 0, 16 * (b - a)))
+        fill(("s3", 224 * q + 32 * (b - a), 224 * q + 32 * (b - a) + 32), 255.0)
+    fill(("tt", 2 * TW, 2 * TW + TRR), 0.0)
+    fill(("pm", 0, 1), 0.0)
+    fill(("zn", 0, 16), 0.0)
+    copy(("klf", 0, 5), ("io40", 0, 5), scale=3.2, bias=c_kl)
+    copy(("kli", 0, 5), ("klf", 0, 5))
+    ts(("kl", 0, 5), ("kli", 0, 5), 15.0, ALU.min, c_h, ALU.add)
+    iota(("bc0", 0, 90), [[0, 3], [32, 6], [4, 5]], E + 15)
+    copy(("bc0", 0, 80), ("bc0", 0, 80), scale=-1.0, bias=c_lh)
     select(("ef", 0, 516), ("ones", 0, 516), [[-1, 516]], ALU.is_equal, 0.0, 3, 4)
     for b in range(4):
-        quant(("eq", "ep"), 128 * b, 128 * b + 128, ("ef", 3 - b, 515 - b))
-    quant(("uq", "up"), 0, 128, ("uin", 0, 512))
+        quant(("eq", "ep"), 128 * b, ("ef", 3 - b, 515 - b))
+    quant(("uq", "up"), 0, ("uin", 0, 512))
     add("V", ("pick", 256), [("uq", 0, 128), ("upo", 0, 16)], [("urq", 0, 256)],
         lambda e: g.vector.tensor_copy(T.urq[:, 0:256].bitcast(dt.uint32),
                                        T.uq[:, 0:128].bitcast(dt.uint32).indirect(T.upo[:, 0:16])))
     add("S", ("pick", 256), [("up", 0, 128), ("upo", 0, 16)], [("urp", 0, 256)],
         lambda e: g.scalar.activation(T.urp[:, 0:256], T.up[:, 0:128].indirect(T.upo[:, 0:16]), ACT.Copy))
-    quant(("nq", "npl"), 0, 128, ("vin", 0, 512))
-    copy(("stf", 0, 2), ("sti", 0, 2))
+    copy(("stf", 0, 2), ("sti", 0, 2), bias=c_lh)
     for t in range(R):
         copy(("bb", 32 * t, 32 * t + 32), ("io40", 0, 32), scale=0.0, bias=("stf", t, t + 1))
     turn(("bt", 0, 64), ("bb", 0, 64))
-    iota(("lb", 0, 4), [[10, 2], [L, 2]], E + 15)
-    iota(("lb", 4, 8), [[5, 4]], 0)
-    copy(("lb", 0, 4), ("lb", 0, 4), bias=c_tl)
-    copy(("lb", 4, 8), ("lb", 4, 8), bias=c_cl)
-    fill(("bs", 0, 48), 0.0)
-    fill(("jf", 0, 48), 0.0)
-    fill(("pm", 0, 512, 256), 0.0)
-    for t in range(R):
-        copy(("bs", 24 * t + 1, 24 * t + 17), ("bt", 32 * t, 32 * t + 32), ind=("off", BO, BO + 1))
-    copy(("bs", 0, 48, 24), ("bs", 1, 48, 24), bias=-float(E))
-    tt(("bd", 0, 48), ("bs", 0, 48), ("t20", 0, 48), ALU.add)
-    tt(("db", 0, 40), ("bs", 2, 42), ("bs", 1, 41), ALU.subtract)
-    ts(("db", 0, 40), ("db", 0, 40), c_r, ALU.add, E + 16.0, ALU.min)
-    copy(("po", 0, 40), ("db", 0, 40))
-    for t in range(R):
-        s = str(t)
-        for e in range(4):
-            copy(("tf" + s, e, 4 * K, 4), ("bt", 32 * t + 16 * (e % 2), 32 * t + 16 * (e % 2) + K), bias=("lb", e, e + 1))
-            copy(("tf" + s, 4 * K + e, 8 * K, 4), ("bs", 24 * t + 2, 24 * t + 17), bias=("lb", 4 + e, 5 + e))
-        copy(("tl" + s, 0, 8 * K), ("tf" + s, 0, 8 * K))
-        if t == 0:
-            fill(("pen" + s, 0, 64 * K), 0.0)
-            fill(("pen" + s, 0, 64 * K, 4), -1e29)
-        else:
-            iota(("pen" + s, 0, 64 * K), [[0, 64 * K]], 0)
-            select(("pen" + s, 0, 64 * K), ("pen" + s, 0, 64 * K), [[0, 16 * K], [1, 4]], ALU.is_gt, -1e29, 0, 0)
-        copy(("pen" + s, 3, 64 * K, 4), ("wpen", 0, 40), ind=("po", 24 * t, 24 * t + K), scale=1e28)
-        tt(("lc" + s, 0, C // 2), ("bd", 24 * t, 24 * t + 24), ("ut" + s, 0, C // 2), ALU.add,
-           ind=("kl", 10 * t, 10 * t + 10))
+    for e in range(1, 4):
+        copy(("bt", 64 * e, 64 * e + 64), ("bt", 0, 64), bias=5.0 * e)
+
+    def lists(t):
+        s, bs = str(t), 16 * t
+        copy(("tl" + s, 0, 64), ("bt", 32 * t, 256), ind=("lam", 0, 4), bias=c_tl)
+        copy(("tl" + s, 64, 128), ("bt", 32 * t, 256), ind=("lam", 4, 8), bias=c_r)
+        copy(("bs", bs, bs + 16), ("bt", 32 * t, 32 * t + 32), ind=("off", BO, BO + 1))
+        tt(("db", bs, bs + K), ("bs", bs + 1, bs + 16), ("bs", bs, bs + K), ALU.subtract)
+        copy(("db", bs, bs + K), ("db", bs, bs + K), bias=c_r)
+        ts(("po", bs, bs + K), ("db", bs, bs + K), 0.0, ALU.max, E + 16.0, ALU.min)
+        for e in range(3):
+            copy(("pen" + s, e, 64 * K, 4), ("ones", 0, 16 * K), scale=0.0 if e else -1e29)
+        copy(("pen" + s, 3, 64 * K, 4), ("wpen", 0, 40), ind=("po", bs, bs + K), scale=1e28)
+        tt(("base" + s, 0, 80), ("bt", 32 * t, 32 * t + 32), ("bc0", 0, 80), ALU.subtract, ind=("kl", 0, 5))
+        copy(("db", bs + K, bs + 16), ("bs", bs, bs + 1), scale=-1.0, bias=c_lh)
+        copy(("wv" + s, 0, 10), ("io40", 0, 10), scale=-4.0, bias=("db", bs + K, bs + 16))
+        copy(("li" + s, 0, 10), ("wv" + s, 0, 10), scale=-4.0, bias=c_r)
+        copy(("dv" + s, 0, PAD), ("ones", 0, PAD), scale=0.0)
 
     def window(t):
         s = str(t)
         head = HEAD if t == 0 else 0
         if head:
             send(1, ("wp", 0, head), ("lp0", 0, head), "lay0")
-        send(1, ("vq" + s, 0, B), ("vq" + s, C, L), "win" + s)
-        send(1, ("vp" + s, 0, B), ("vp" + s, C, L), "win" + s)
-        arrival(1, [("vq" + s, C, L), ("vp" + s, C, L)], "win" + s, 2)
+        send(1, ("vq" + s, B, 2 * B), ("vq" + s, 0, B), "win" + s)
+        send(1, ("vp" + s, B, 2 * B), ("vp" + s, 0, B), "win" + s)
+        arrival(1, [("vq" + s, 0, B), ("vp" + s, 0, B)], "win" + s, 2)
         send(1 + t, ("wp", head, 512), ("lp" + s, head, 512), "lay" + s)
         send(1 + t, ("wq", 0, 512), ("lq" + s, 0, 512), "lay" + s)
         arrival(1 + t, [("lq" + s, 0, 512), ("lp" + s, 0, 512)], "lay" + s, 3 if head else 2)
 
-    quant(("vq0", "vp0"), 0, 128, ("xin", 0, a0))
-    window(0)
-    quant(("vq0", "vp0"), 128, C, ("xin", a0, 4 * C))
-    fill(("off", F2, F2 + 1), 15)
-    fill(("nn", 0, 32, 16), 0)
-    fill(("jf", 1, 48, 24), -16.0)
-    iota(("tab", 0, 16), [[16, 16]], 32)
-    copy(("tab", 0, 16), ("tab", 0, 16), bias=c_h)
-    iota(("par", 0, 48), [[0, 24], [16, 2]], 0)
-    tt(("par", 0, 48), ("par", 0, 48), ("bs", 0, 48), ALU.add)
     EB = ("eq", "ep")
 
-    def unpack(t, piece, bank):
-        a, b, keep = PIECE[t][piece]
+    def unpack(t, a, b, keep, x, n):
         V = ("vq%d" % t, "vp%d" % t)
         for h in range(2):
-            ps = 2 * piece + h
-            mm(ps, ("urq", "urp"), V, a, b, 128 * h)
-            copy(("sc%d" % t, L * h + keep, L * h + b), ("ps%d" % ps, keep - a, b - a))
+            product(("sc%d" % t, L * h + x, L * h + x + n), [(("urq", "urp"), 128 * h, V)], a, b, keep)
         for bb in range(4):
-            ps = bank + (bb + 2) % 4
-            mm(ps, EB, V, a, b, 128 * bb)
-            copy(("dv%d" % t, 4 * keep + bb, 4 * b, 4), ("ps%d" % ps, keep - a, b - a), scale=0.5)
+            product(("dv%d" % t, PAD + 4 * x + bb, PAD + 4 * (x + n), 4), [(EB, 128 * bb, V)], a, b, keep, 0.5)
 
-    unpack(0, 0, 4)
+    lists(0)
+    quant(("vq0", "vp0"), B, ("xin", 0, a0))
+    window(0)
+    quant(("vq0", "vp0"), B + 128, ("xin", a0, 4 * C))
+    unpack(0, B, L, 0, 0, C)
     for t in range(R):
         s, s2 = str(t), str(t + 1)
         Z, H, X = ("zq" + s, "zp" + s), ("hq" + s, "hp" + s), ("vq" + s2, "vp" + s2)
-        unpack(t, 1, 4)
-        win = ("sc" + s, 0, 2 * L)
-        for a, b in zip(FINE[t], FINE[t][1:]):
-            tp, tb, dd, aa, s1, pen = [(n + s, 64 * a, 64 * b) for n in ("tp", "tb", "dd", "aa", "s1", "pen")]
-            copy(tp, win, ind=("tl" + s, 4 * a, 4 * b))
-            turn(tb, tp)
-            tt(dd, win, tb, ALU.subtract, ind=("tl" + s, 4 * K + 4 * a, 4 * K + 4 * b))
-            absol(aa, dd, ("off", PM, PM + 4 * (b - a)))
-            scan(s1, pen, aa, ALU.add, ALU.max)
-        for a, b in zip(COARSE[t], COARSE[t][1:]):
-            dist, pm = ("s1" + s, 64 * a + 3, 64 * b, 4), 256 * t
-            scan(("pm", pm + 16 * a + 1, pm + 16 * b + 1), ("rst", 16 * a, 16 * b), dist, ALU.max, ALU.min)
-            tt(("nr" + s, 16 * a, 16 * b), dist, ("pm", pm + 16 * a, pm + 16 * b), ALU.is_ge)
-            scan(("s3" + s, 16 * a, 16 * b), ("nr" + s, 16 * a, 16 * b), ("kt", 16 * a, 16 * b), ALU.mult, ALU.max)
-            copy(("bc" + s, 32 * a, 32 * b), ("s3" + s, 16 * a, 16 * b), ind=("off", BC, BC + 2 * (b - a)))
-            turn(("rr" + s, 32 * a, 32 * b), ("bc" + s, 32 * a, 32 * b))
-            nf, nn = ("nf", 16 * t + a + 1, 16 * t + b + 1), ("nn", 16 * t + a + 1, 16 * t + b + 1)
-            tt(nf, ("s3" + s, 16 * a + 15, 16 * b, 16), ("tab", a, b), ALU.add)
-            copy(nn, nf)
-            copy(("g2" + s, 16 * a, 16 * b), ("rr" + s, 0, 32 * b), ind=("nn", 16 * t + a, 16 * t + b))
-        ch, g2 = "ch" + s, "g2" + s
-        ts((ch, 1, 17), ("rr" + s, 0, 32), 0.0, ALU.add, ind=("off", FO, FO + 1))
-        ts((ch, 17, 33), (g2, 16, 32), 0.0, ALU.add, ind=("off", F2, F2 + 1))
-        for k in range(1, K, 2):
-            w = min(2, K - 1 - k)
-            ts((ch, 16 * k + 17, 16 * (k + w) + 17), (g2, 16 * k + 16, 16 * (k + w) + 16), -16.0 * (k + 1), ALU.add,
-               ind=(ch, 16 * k, 16 * k + w))
-        for i, (a, b) in enumerate(((0, CUT[t]), (CUT[t], C))):
-            ka, kb = (0, (b - 1) // E) if i == 0 else ((a - 1) // E, K)
-            n, la, lb = b - a, a // 2, b // 2
-            copy(("jf", 24 * t + ka + 2, 24 * t + kb + 2), (ch, 16 * ka + 16, 16 * kb + 16, 16), scale=-1.0, bias=15.0)
-            tt(("l2" + s, la, lb), ("jf", 24 * t, 24 * t + kb + 2), ("lc" + s, la, lb), ALU.add,
-               ind=("kl", 10 * t + la // 16, 10 * t + lb // 16))
-            copy(("li" + s, la, lb), ("l2" + s, la, lb), scale=4.0)
-            dw = ("dv" + s, 0, 4 * L)
-            for c, d in zip(PICKS[t], PICKS[t][1:]):
-                if a <= c < b:
-                    o = la + (c - a) // 4
-                    copy(("zn" + s, 4 * c, 4 * d), dw, ind=("li" + s, o + n // 4, o + n // 4 + (d - c) // 4))
-                    tt(("zt" + s, 4 * c, 4 * d), dw, ("zn" + s, 4 * c, 4 * d), ALU.add, ind=("li" + s, o, o + (d - c) // 4))
-            quant(Z, a, b, ("zt" + s, 4 * a, 4 * b))
+        tag[0] = s + "n"
+        unpack(t, 0, 128, 0, C, B)
+        win, wv, li = ("sc" + s, 0, 2 * L), "wv" + s, "li" + s
+        state = ("off", FO, FO + 1)
+        for q, (a, b) in enumerate(CHUNK):
+            n, tab, s3 = b - a, TW * q, 224 * q
+            tag[0] = s + "c" + str(q)
+            for i in range(SUB[t][q]):
+                c, d = 4 * a + 4 * n * i // SUB[t][q], 4 * a + 4 * n * (i + 1) // SUB[t][q]
+                tp, tb, dd = [(x, 16 * c, 16 * d) for x in ("tp", "tb", "dd")]
+                copy(tp, win, ind=("tl" + s, c, d))
+                turn(tb, tp)
+                tt(dd, win, tb, ALU.subtract, ind=("tl" + s, 64 + c, 64 + d))
+            for e in range(4):
+                absol(("aa", 64 * a + e, 64 * b, 4), ("dd", 64 * a + 16 * n * e, 64 * a + 16 * n * (e + 1)))
+            scan(("s1", 64 * a, 64 * b), ("pen" + s, 64 * a, 64 * b), ("aa", 64 * a, 64 * b), ALU.add, ALU.max)
+            dist = ("s1", 64 * a + 3, 64 * b, 4)
+            scan(("pm", 16 * a + 1, 16 * b + 1), ("rst", 0, 16 * n), dist, ALU.max, ALU.min)
+            tt(("nr", 32 * a, 32 * b, 2), dist, ("pm", 16 * a, 16 * b), ALU.is_ge)
+            scan(("s3", s3, s3 + 32 * n), ("nr", 32 * a, 32 * b), ("kt", 0, 32 * n), ALU.mult, ALU.max)
+            scan(("bc", 32 * a, 32 * b), ("rs2", 0, 32 * n), ("s3", s3 + 31, s3 + 31 + 32 * n), ALU.max, ALU.min)
+            rr = ("tt", tab + TRR, tab + TRR + 32 * n)
+            turn(rr, ("bc", 32 * a, 32 * b))
+            g2 = ("tt", tab + TG2, tab + TG2 + 32 * (n - 1))
+            copy(("nn", 2 * a, 2 * b - 2), ("bc", 32 * a, 32 * b - 32, 16), bias=c_nn)
+            copy(g2, rr, ind=("nn", 2 * a, 2 * b - 2))
+            for i in range(n // 3):
+                copy(("tt", tab + 16 * i, tab + 16 * i + 16), g2, ind=("nn", 2 * a + 6 * i, 2 * a + 6 * i + 1))
+            for i in range(a // 3, b // 3):
+                tabs = ("tt", tab, tab + TRR + 32 * n)
+                now = state
+                if 3 * i + 3 < K:
+                    ts(("ch", 16 * i, 16 * i + 16), tabs, ("cc", i, i + 1), ALU.add, ind=now)
+                    state = ("ch", 16 * i + 10, 16 * i + 11)
+                tt((wv, 10 + 15 * i, 26 + 15 * i), tabs, ("base" + s, 15 * i, 15 * i + 16), ALU.subtract, ind=now)
+        part = lambda c: s + str(sum(4 * c >= x[2] for x in PIECE[t][:-1]))
+        for c, d in zip(LI[t][1:], LI[t][2:]):
+            tag[0] = part(c - 5)
+            copy((li, c, d), (wv, c, d), scale=-4.0, bias=c_r)
+        for c, d in zip(ZN[t], ZN[t][1:]):
+            tag[0] = part(c)
+            copy(("zn", 16 * c + 16, 16 * d + 16), ("dv" + s, PAD, PAD + 4 * L), ind=(li, c, d))
+        for c, d in zip(ZT[t], ZT[t][1:]):
+            tag[0] = part(c)
+            tt(("zt" + s, 16 * c + 16, 16 * d + 16), ("dv" + s, 0, PAD + 4 * L), ("zn", 16 * c + 16, 16 * d + 16),
+               ALU.add, ind=(li, c + 5, d + 5))
+        copy(("pout", 16 * t, 16 * t + 16), (wv, 5, 85, 5), scale=-1.0, bias=-float(E))
+        end = 0
+        for i, (a, new, b) in enumerate(PIECE[t]):
+            at, end = end, end + b - a
+            tag[0] = s + str(i)
+            j = quant(Z, at, ("zt" + s, 4 * a + 16, 4 * b + 16))
+            if b == C and t + 1 < R:
+                behind[0], tag[0] = [j], ""
+                lists(t + 1)
+                quant(("nq", "npl"), 0, ("vin", 0, 512))
+                behind[0], tag[0] = [], s + str(i)
             for bb in range(4):
-                mm(bb, ("lq" + s, "lp" + s), Z, a, b, 128 * bb)
+                product(("ht" + s, 4 * new + bb, 4 * b, 4), [(("lq" + s, "lp" + s), 128 * bb, Z)], at, end, new - a,
+                        0.03125)
+            quant(H, at, ("ht" + s, 4 * a, 4 * b))
             for bb in range(4):
-                mm(4 + bb, EB, Z, a, b, 128 * bb, True, False)
-            for bb in range(4):
-                copy(("ht" + s, 4 * a + bb, 4 * b, 4), ("ps%d" % bb, 0, n), scale=0.03125)
-            quant(H, a, b, ("ht" + s, 4 * a, 4 * b))
-            for bb in range(4):
-                mm(4 + bb, EB, H, a, b, 128 * bb, False, True)
-            for bb in range(4):
-                copy(("xt" + s, 4 * a + bb, 4 * b, 4), ("ps%d" % (4 + bb), 0, n))
-            quant(X, a, b, ("xt" + s, 4 * a, 4 * b))
-            if t + 1 == R:
-                dma(T.oc[:, 4 * a:4 * b], u8(("vq2", a, b)), [("vq2", a, b)], [], 4 * n)
-            elif i == 0:
-                window(t + 1)
-                unpack(t + 1, 0, 0)
-        tt(("pout", 16 * t, 16 * t + 16), ("jf", 24 * t + 1, 24 * t + 17), ("par", 24 * t + 1, 24 * t + 17), ALU.add)
+                j = product(("xt" + s, 4 * new + bb, 4 * b, 4), [(EB, 128 * bb, Z), (EB, 128 * bb, H)], at, end, new - a)
+                ops[j]["extra"] = AHEAD * (len(PIECE[t]) - 1 - i)
+            if t + 1 < R:
+                quant(X, B + at, ("xt" + s, 4 * a, 4 * b))
+                if i == 0:
+                    window(t + 1)
+                unpack(t + 1, B + at, B + end, new - a, new, b - new)
+            else:
+                quant(X, a, ("xt" + s, 4 * a, 4 * b))
+                keep = PIECE[t][i + 1][0] if i + 1 < len(PIECE[t]) else b
+                dma(T.oc[:, 4 * a:4 * keep], u8(("vq2", a, keep)), [("vq2", a, keep)], [], 4 * (keep - a))
+                product(("ysb", new, b), [(("nq", "npl"), 0, X)], a, b, new - a)
+                dma(T.y[:, new:b], T.ysb[:, new:b], [("ysb", new, b)], [], 4 * (b - new))
     dma(T.ol[:], T.pout[0:128:16, 0:32], [("pout", 0, 32)], [], 8)
-    for i, (a, b) in enumerate(((0, CUT[-1]), (CUT[-1], C))):
-        mm(i, ("nq", "npl"), ("vq2", "vp2"), a, b)
-        copy(("ysb", a, b), ("ps%d" % i, 0, b - a))
-        dma(T.y[:, a:b], T.ysb[:, a:b], [("ysb", a, b)], [], 4 * (b - a))
     for k in range(4):
         dma(T.osc[4 * k:4 * k + 4, 0:C], T.vp2[32 * k:32 * k + 4, 0:C], [("vp2", 0, C)], [], 10)
-    return ops
+    return ops, bank
 
 
 def depend(ops):
@@ -369,28 +389,148 @@ def depend(ops):
         deps = {}
         for wr, rs in ((False, o["reads"]), (True, o["writes"])):
             for r in rs:
-                bank = SCRATCH[r[0]][0] == "psum"
-                cols = None if bank else set(range(*r[1:]))
+                cols = set(range(*r[1:]))
                 for j, w, c in seen.get(r[0], []):
-                    if j != i and (bank or ((wr or w) and not cols.isdisjoint(c))):
-                        deps[j] = not (bank and o.get("acc"))
-                if bank:
-                    seen[r[0]] = []
+                    if j != i and (wr or w) and not cols.isdisjoint(c):
+                        deps[j] = not (r[0][0] == "@" and o.get("acc"))
                 seen.setdefault(r[0], []).append((i, wr, cols))
         for j in o["after"]:
             deps.setdefault(j, False)
         o["deps"] = deps
 
 
+NOMINAL = dict(cycle=1.05e-3, pick=1.56, wake=0.18, pe=0.6e-3, dma=1.6, issue=0.3, local=180e3, first=1.0,
+               remote=1.5, link=60e3, lean=0.6)
+LEAN = {"": 0, "tp": 0, "tt": 0.2, "dv": 3, "ht": 0.1, "ht00": 0.2, "xt": 0.05, "xt00": 0, "xt10": 0.1}
+BUMP = {"ef": 0.5, "aa": -0.5, "ch": -1, "dv": -1, "hq": -0.5, "xt": -0.25, "0c0": -1, "02": 0.5, "10": -0.5}
+GAP = {"0c0": 0.25, "0c1": 0.2, "0c2": 0.25, "02": 0.13, "1c0": 0.2, "1c1": 0.3, "1c2": 0.3}
+
+
+def cost(o, e, P):
+    k, n = o["size"]
+    c = P["cycle"]
+    if k == "pick":
+        return (60 if e == "V" else 78) * c + n * P["pick"] * c
+    if k in ("half", "one", "two"):
+        return max(64, n * (2 if k == "two" else 0.5 if k == "half" and e == "V" else 1)) * c
+    if k == "quant":
+        return (15 + 0.265 * n) * c
+    if k == "mm":
+        return (n + 16) * P["pe"]
+    if k == "pool":
+        return (180 + 2 * n) * c
+    return P["issue"] if k != "arrive" else 0.0
+
+
+def place(ops, bank, P=NOMINAL, rank=None):
+    wake = P["wake"]
+
+    def name(o):
+        return o["writes"][0][0][:2] if o["kind"] == "op" else ""
+
+    def tail(o):
+        k, n = o["size"]
+        return P["dma"] + 128 * n / P["local"] if k == "dma" else P["remote"] + 128 * n / P["link"] if k == "send" else 0.0
+
+    for o in ops:
+        o["rest"], o["end"], o["users"] = 0.0, None, []
+    for o in reversed(ops):
+        o["rest"] += cost(o, o["on"][0], P) + tail(o) + o.get("extra", 0.0)
+        for j, hard in o["deps"].items():
+            gap = wake if hard else -tail(ops[j]) if o["kind"] != "arrive" else 0.0
+            ops[j]["rest"] = max(ops[j]["rest"], o["rest"] + gap)
+    need = {}
+    for i, o in enumerate(ops):
+        if o["kind"] != "mm":
+            need[i] = {j for m in o["mms"] + [i] for j in ops[m]["deps"]} - set(o["mms"])
+            for j in need[i]:
+                ops[j]["users"].append(i)
+    rank = rank or {i: -ops[i]["rest"] - BUMP.get(ops[i]["tag"], 0.0) - BUMP.get(name(ops[i]), 0.0) for i in need}
+    ready = [i for i in need if not need[i]]
+    busy = {e: [] for e in list("VSPGYA") + list(range(8))}
+    link, plan = [0.0, P["first"]], []
+
+    def after(o):
+        t = 0.0
+        for j, hard in o["deps"].items():
+            if ops[j]["end"] is not None:
+                t = max(t, ops[j]["end"] + GAP.get(o["tag"], wake) if hard
+                        else ops[j]["end" if o["kind"] == "arrive" else "issued"])
+        return t
+
+    def fit(e, t, d):
+        for a, b, _ in busy[e]:
+            if t + d <= a + 1e-9:
+                break
+            t = max(t, b)
+        return t
+
+    def hold(e, t, d, i):
+        busy[e].append((t, t + d, i))
+        busy[e].sort()
+
+    def slot(o, e):
+        d, t = cost(o, e, P) + (link[1] if o["kind"] == "send" else 0.0), after(o)
+        if not o["mms"]:
+            return fit(e, t, d), None, None
+        dm, first = cost(ops[o["mms"][0]], "P", P), after(ops[o["mms"][0]])
+        at = max(after(ops[o["mms"][-1]]), first + dm * (len(o["mms"]) - 1))
+        while True:
+            at = fit("P", at, dm)
+            s = fit(e, max(t, at + dm + wake), d)
+            for m in (at, s - wake - dm):
+                ms = [m]
+                if len(o["mms"]) == 2:
+                    ms = [max([x - dm for x in [m] + [a for a, _, _ in busy["P"] if a < m]
+                               if x - dm >= first and fit("P", x - dm, dm) == x - dm], default=None), m]
+                if ms[0] is None or fit("P", m, dm) != m:
+                    continue
+                for b in range(8):
+                    if fit(b, ms[0], s + d + wake - ms[0]) == ms[0]:
+                        return s, ms, b
+            at = min([x[1] for b in range(8) for x in busy[b] if x[1] > at] + [at + dm])
+
+    while ready:
+        i = min(ready, key=lambda i: rank[i])
+        o = ops[i]
+        lean = LEAN.get(name(o) + o["tag"], LEAN.get(name(o), P["lean"]))
+        _, e, (t, m, b) = min((x[0] + cost(o, e, P) + lean * k, e, x)
+                              for k, e in enumerate(o["on"]) for x in [slot(o, e)])
+        d = cost(o, e, P)
+        if o["mms"]:
+            bank[o["reads"][0][0]] = b
+            hold(b, m[0], t + d + wake - m[0], i)
+            for j, at in zip(o["mms"], m):
+                hold("P", at, cost(ops[j], "P", P), j)
+                plan.append((at, "P", j))
+                ops[j]["end"] = ops[j]["issued"] = at + cost(ops[j], "P", P)
+        if o["kind"] == "send":
+            d, link[1] = d + link[1], 0.0
+            link[0] = max(link[0], t + d) + tail(o) - P["remote"]
+        o["issued"], o["end"] = t + d, link[0] + P["remote"] if o["kind"] == "send" else t + d + tail(o)
+        hold(e, t, d, i)
+        plan.append((t, e, i))
+        ready.remove(i)
+        for j in o["mms"] + [i]:
+            for u in ops[j]["users"]:
+                need[u].discard(j)
+                if not need[u]:
+                    ready.append(u)
+    for b in range(8):
+        for x, y in zip(busy[b], busy[b][1:]):
+            ops[ops[y[2]]["mms"][0]]["deps"][x[2]] = True
+    return [(e, i) for _, e, i in sorted(plan)]
+
+
 def rank_program(g, core, T, topo):
     if T.rank_of(core) is None:
         return
-    ops = build(g, T, topo, core)
+    ops, bank = build(g, T, topo, core)
     depend(ops)
+    plan = place(ops, bank)
     queue = {"V": g.vector, "S": g.scalar, "P": g.tensor, "G": g, "Y": g.sync}
     known = {e: {} for e in queue}
     count, waited = {}, {}
-    plan = [(w[0], int(w[1:])) for w in ORDER.split()] or [(o["on"][0], i) for i, o in enumerate(ops)]
     for at, (e, i) in enumerate(plan):
         o = ops[i]
         o["at"] = at

@@ -4,11 +4,11 @@ C, E, B, R = 320, 20, 112, 2
 L = C + B
 K = 15
 CHUNK = ((0, 6), (6, 12), (12, 15))
-SUB = ((3, 4, 1), (2, 2, 2))
+SUB = ((3, 3, 1), (3, 2, 2))
 PIECE = (((0, 0, 132), (132, 132, 260), (192, 260, C)), ((0, 0, 188), (188, 188, C)))
-ZN = ((0, 24, 40, 58, 80), (0, 10, 34, 48, 70, 80))
-ZT = ((-1, 19, 33, 49, 65, 80), (-1, 5, 33, 47, 65, 80))
-LI = ((0, 10, 25, 40, 70, 85), (0, 10, 40, 55, 70, 85))
+ZN = ((0, 24, 38, 58, 80), (0, 6, 10, 28, 36, 46, 60, 70, 80))
+ZT = ((-1, 19, 33, 43, 49, 65, 75, 80), (-1, 7, 33, 47, 53, 59, 65, 80))
+LI = ((0, 10, 25, 40, 70, 85), (0, 10, 40, 70, 85))
 AHEAD = 1.2
 HEAD = 128
 PAD = 4 * E
@@ -19,20 +19,20 @@ SCRATCH = {}
 for _n, _w, _d in (("xin", 4 * C, BF), ("uin", 512, BF), ("vin", 512, BF), ("sti", 2, I32), ("wq", 512, Q4),
                    ("wp", 512, U8), ("uq", 128, Q4), ("up", 128, U8), ("urq", 256, Q4), ("urp", 256, U8),
                    ("nq", 128, Q4), ("npl", 128, U8), ("ones", 516, BF), ("ef", 516, BF), ("eq", 512, Q4),
-                   ("ep", 512, U8), ("pi", 2, I32), ("ai", 8, I32), ("af", 24, F32), ("io40", 40, F32),
+                   ("ep", 512, U8), ("pi", 2, I32), ("ai", 8, I32), ("af", 24, F32), ("count", 40, F32),
                    ("wpen", 40, F32), ("lf", 48, F32), ("upo", 16, U16), ("off", 24, U16), ("items", 128, F32),
                    ("il", 256, F32), ("it", 256, F32), ("lam", 8, U16), ("kli", 6, I32), ("klf", 6, F32),
                    ("kl", 6, U16), ("kt", 192, BF), ("rst", 96, F32), ("rs2", 192, BF), ("stf", 2, F32),
                    ("bb", 64, F32), ("bt", 256, F32), ("bs", 32, F32), ("db", 32, F32), ("po", 32, U16),
-                   ("bc0", 90, F32), ("cc", 8, F32), ("nn", 32, U16),
+                   ("bc0", 120, F32), ("cc", 8, F32), ("nn", 32, U16),
                    ("tp", 64 * K, F32), ("tb", 64 * K, F32), ("dd", 64 * K, F32), ("aa", 64 * K, F32),
                    ("s1", 64 * K, F32), ("pm", 256, F32), ("nr", 32 * K, BF), ("s3", 3 * 224, BF),
-                   ("bc", 32 * K, BF), ("tt", 3 * TW, BF), ("ch", 64, U16), ("zn", 4 * C + 16, F32),
+                   ("bc", 32 * K, BF), ("tt", 3 * TW, BF), ("ch", 96, U16), ("zn", 4 * C + 16, F32),
                    ("pout", 32, F32), ("ysb", C, F32), ("vq2", C, Q4), ("vp2", C, U8)):
     SCRATCH[_n] = ("sbuf", [128, _w], _d)
 for _t in range(R):
     for _n, _w, _d in (("vq", 512, Q4), ("vp", 512, U8), ("lq", 512, Q4), ("lp", 512, U8), ("sc", 2 * L, F32),
-                       ("dv", PAD + 4 * L, F32), ("tl", 128, U16), ("pen", 64 * K, BF), ("base", 80, F32),
+                       ("dv", PAD + 4 * L, F32), ("tl", 128, U16), ("pen", 64 * K, BF), ("base", 96, F32),
                        ("wv", 96, F32), ("li", 96, U16), ("zt", 4 * C + 16, BF), ("zq", 388, Q4), ("zp", 388, U8),
                        ("ht", 4 * C, BF), ("hq", 388, Q4), ("hp", 388, U8), ("xt", 4 * C, BF)):
         SCRATCH["%s%d" % (_n, _t)] = ("sbuf", [128, _w], _d)
@@ -127,9 +127,6 @@ def build(g, T, topo, core):
             return g.iota(ap(o), pat, base, cm, allow_small_or_imprecise_dtypes=True)
         return add("G", ("pool", cnt(o)), [], [o], emit)
 
-    def select(o, i, pat, op, other, base, cm):
-        return add("G", ("pool", cnt(o)), [i], [o], lambda e: g.affine_select(ap(o), ap(i), pat, op, other, base, cm))
-
     def quant(q, a, i):
         b = a + cnt(i) // 4
         c, p = (q[0], a, b), (q[1], a, b)
@@ -174,14 +171,12 @@ def build(g, T, topo, core):
             inc=calls * len(topo.engines(cores[(rank + step) % n_r], core)))
 
     a0 = 4 * 128
-    dma(T.xin[:, 0:a0], T.x[:, 0:a0], [], [("xin", 0, a0)], 2 * a0)
-    dma(T.wp[:, 0:HEAD], T.ws[:, 0:HEAD], [], [("wp", 0, HEAD)], HEAD)
-    dma(T.sti[:], T.st[:], [], [("sti", 0, 2)], 8)
-    dma(T.uin[:], T.u[:], [], [("uin", 0, 512)], 1024)
-    dma(T.xin[:, a0:4 * C], T.x[:, a0:4 * C], [], [("xin", a0, 4 * C)], 8 * C - 2 * a0)
-    dma(T.wp[:, HEAD:512], T.ws[:, HEAD:512], [], [("wp", HEAD, 512)], 512 - HEAD)
-    dma(u8(("wq", 0, 512)), T.wc[:], [], [("wq", 0, 512)], 2048)
-    dma(T.vin[:], T.v[:], [], [("vin", 0, 512)], 1024)
+    for i, j in enumerate((dma(T.wp[:, 0:HEAD], T.ws[:, 0:HEAD], [], [("wp", 0, HEAD)], HEAD),
+                           dma(T.sti[:], T.st[:], [], [("sti", 0, 2)], 8),
+                           dma(T.xin[:, 0:a0], T.x[:, 0:a0], [], [("xin", 0, a0)], 2 * a0),
+                           dma(T.uin[:], T.u[:], [], [("uin", 0, 512)], 1024),
+                           dma(T.xin[:, a0:4 * C], T.x[:, a0:4 * C], [], [("xin", a0, 4 * C)], 8 * C - 2 * a0))):
+        ops[j]["extra"] = 5.0 - i
 
     iota(("pi", 0, 1), [[0, 1]], 0, 1)
     for j, m in enumerate((15, 16, 1)):
@@ -221,8 +216,8 @@ def build(g, T, topo, core):
     turn(("it", 0, 256), ("il", 0, 256))
     copy(("lam", 0, 4), ("it", 0, 128, 32))
     copy(("lam", 4, 8), ("it", 128, 256, 32), bias=1.0)
-    iota(("io40", 0, 40), [[1, 40]], 0)
-    ts(("wpen", 0, 40), ("io40", 0, 40), c_r, ALU.add, E + 15.0, ALU.is_equal)
+    iota(("count", 0, 40), [[1, 40]], 0)
+    ts(("wpen", 0, 40), ("count", 0, 40), c_r, ALU.add, E + 15.0, ALU.is_equal)
     fill(("ones", 0, 516), 1.0)
     iota(("kt", 0, 192), [[32, 6], [-1, 16], [-256, 2]], 15)
     fill(("rst", 0, 96), 0.0)
@@ -235,12 +230,13 @@ def build(g, T, topo, core):
     fill(("tt", 2 * TW, 2 * TW + TRR), 0.0)
     fill(("pm", 0, 1), 0.0)
     fill(("zn", 0, 16), 0.0)
-    copy(("klf", 0, 5), ("io40", 0, 5), scale=3.2, bias=c_kl)
+    copy(("klf", 0, 5), ("count", 0, 5), scale=3.2, bias=c_kl)
     copy(("kli", 0, 5), ("klf", 0, 5))
     ts(("kl", 0, 5), ("kli", 0, 5), 15.0, ALU.min, c_h, ALU.add)
     iota(("bc0", 0, 90), [[0, 3], [32, 6], [4, 5]], E + 15)
     copy(("bc0", 0, 80), ("bc0", 0, 80), scale=-1.0, bias=c_lh)
-    select(("ef", 0, 516), ("ones", 0, 516), [[-1, 516]], ALU.is_equal, 0.0, 3, 4)
+    add("G", ("pool", 516), [("ones", 0, 516)], [("ef", 0, 516)],
+        lambda e: g.affine_select(T.ef[:, 0:516], T.ones[:, 0:516], [[-1, 516]], ALU.is_equal, 0.0, 3, 4))
     for b in range(4):
         quant(("eq", "ep"), 128 * b, ("ef", 3 - b, 515 - b))
     quant(("uq", "up"), 0, ("uin", 0, 512))
@@ -251,7 +247,7 @@ def build(g, T, topo, core):
         lambda e: g.scalar.activation(T.urp[:, 0:256], T.up[:, 0:128].indirect(T.upo[:, 0:16]), ACT.Copy))
     copy(("stf", 0, 2), ("sti", 0, 2), bias=c_lh)
     for t in range(R):
-        copy(("bb", 32 * t, 32 * t + 32), ("io40", 0, 32), scale=0.0, bias=("stf", t, t + 1))
+        copy(("bb", 32 * t, 32 * t + 32), ("count", 0, 32), scale=0.0, bias=("stf", t, t + 1))
     turn(("bt", 0, 64), ("bb", 0, 64))
     for e in range(1, 4):
         copy(("bt", 64 * e, 64 * e + 64), ("bt", 0, 64), bias=5.0 * e)
@@ -269,7 +265,7 @@ def build(g, T, topo, core):
         copy(("pen" + s, 3, 64 * K, 4), ("wpen", 0, 40), ind=("po", bs, bs + K), scale=1e28)
         tt(("base" + s, 0, 80), ("bt", 32 * t, 32 * t + 32), ("bc0", 0, 80), ALU.subtract, ind=("kl", 0, 5))
         copy(("db", bs + K, bs + 16), ("bs", bs, bs + 1), scale=-1.0, bias=c_lh)
-        copy(("wv" + s, 0, 10), ("io40", 0, 10), scale=-4.0, bias=("db", bs + K, bs + 16))
+        copy(("wv" + s, 0, 10), ("count", 0, 10), scale=-4.0, bias=("db", bs + K, bs + 16))
         copy(("li" + s, 0, 10), ("wv" + s, 0, 10), scale=-4.0, bias=c_r)
         copy(("dv" + s, 0, PAD), ("ones", 0, PAD), scale=0.0)
 
@@ -281,9 +277,18 @@ def build(g, T, topo, core):
         send(1, ("vq" + s, B, 2 * B), ("vq" + s, 0, B), "win" + s)
         send(1, ("vp" + s, B, 2 * B), ("vp" + s, 0, B), "win" + s)
         arrival(1, [("vq" + s, 0, B), ("vp" + s, 0, B)], "win" + s, 2)
+
+    def layer(t):
+        s = str(t)
+        head = HEAD if t == 0 else 0
+        if head:
+            dma(T.wp[:, HEAD:512], T.ws[:, HEAD:512], [("urq", 0, 1)], [("wp", HEAD, 512)], 512 - HEAD)
+            dma(u8(("wq", 0, 512)), T.wc[:], [("urq", 0, 1)], [("wq", 0, 512)], 2048)
         send(1 + t, ("wp", head, 512), ("lp" + s, head, 512), "lay" + s)
         send(1 + t, ("wq", 0, 512), ("lq" + s, 0, 512), "lay" + s)
         arrival(1 + t, [("lq" + s, 0, 512), ("lp" + s, 0, 512)], "lay" + s, 3 if head else 2)
+        if head:
+            dma(T.vin[:], T.v[:], [("lq0", 0, 1)], [("vin", 0, 512)], 1024)
 
     EB = ("eq", "ep")
 
@@ -299,6 +304,7 @@ def build(g, T, topo, core):
     window(0)
     quant(("vq0", "vp0"), B + 128, ("xin", a0, 4 * C))
     unpack(0, B, L, 0, 0, C)
+    layer(0)
     for t in range(R):
         s, s2 = str(t), str(t + 1)
         Z, H, X = ("zq" + s, "zp" + s), ("hq" + s, "hp" + s), ("vq" + s2, "vp" + s2)
@@ -370,6 +376,7 @@ def build(g, T, topo, core):
                 quant(X, B + at, ("xt" + s, 4 * a, 4 * b))
                 if i == 0:
                     window(t + 1)
+                    layer(t + 1)
                 unpack(t + 1, B + at, B + end, new - a, new, b - new)
             else:
                 quant(X, a, ("xt" + s, 4 * a, 4 * b))
@@ -399,11 +406,13 @@ def depend(ops):
         o["deps"] = deps
 
 
-NOMINAL = dict(cycle=1.05e-3, pick=1.56, wake=0.18, pe=0.6e-3, dma=1.6, issue=0.3, local=180e3, first=1.0,
-               remote=1.5, link=60e3, lean=0.6)
-LEAN = {"": 0, "tp": 0, "tt": 0.2, "dv": 3, "ht": 0.1, "ht00": 0.2, "xt": 0.05, "xt00": 0, "xt10": 0.1}
-BUMP = {"ef": 0.5, "aa": -0.5, "ch": -1, "dv": -1, "hq": -0.5, "xt": -0.25, "0c0": -1, "02": 0.5, "10": -0.5}
-GAP = {"0c0": 0.25, "0c1": 0.2, "0c2": 0.25, "02": 0.13, "1c0": 0.2, "1c1": 0.3, "1c2": 0.3}
+NOMINAL = dict(cycle=1.05e-3, pick=1.56, wake=0.2, pe=0.6e-3, dma=1.2, issue=0.15, local=180e3, first=1.0,
+               remote=0.7, link=100e3, lean=0.6)
+LEAN = {"": 0, "tp": 0, "tt": 0.2, "dv": 0.05, "ht11": 0, "xt00": 0.05, "xt11": 0}
+BUMP = {"eq": -2, "kt": -1, "sc": -0.25, "tp": 1, "tb": 0.5, "aa": -0.5, "wv": -1,
+        "0n": -1, "0c0": -1, "tt0c1": -2, "tp0c2": -0.25, "dd0c2": 0.25, "xt01": 2, "02": 0.5,
+        "tt1c0": -1, "tp1c1": -1, "1c2": 0.25, "tp1c2": -2, "zn10": -1, "ht10": -2}
+GAP = {"0c0": 0.25, "0c2": 0.25, "00": 0.25, "02": 0.25, "1c0": 0.25, "1c1": 0.3, "1c2": 0.3, "10": 0.16, "11": 0.16}
 
 
 def cost(o, e, P):
@@ -445,7 +454,8 @@ def place(ops, bank, P=NOMINAL, rank=None):
             need[i] = {j for m in o["mms"] + [i] for j in ops[m]["deps"]} - set(o["mms"])
             for j in need[i]:
                 ops[j]["users"].append(i)
-    rank = rank or {i: -ops[i]["rest"] - BUMP.get(ops[i]["tag"], 0.0) - BUMP.get(name(ops[i]), 0.0) for i in need}
+    rank = rank or {i: -ops[i]["rest"] - BUMP.get(ops[i]["tag"], 0.0)
+                    - BUMP.get(name(ops[i]) + ops[i]["tag"], BUMP.get(name(ops[i]), 0.0)) for i in need}
     ready = [i for i in need if not need[i]]
     busy = {e: [] for e in list("VSPGYA") + list(range(8))}
     link, plan = [0.0, P["first"]], []
@@ -479,15 +489,17 @@ def place(ops, bank, P=NOMINAL, rank=None):
             at = fit("P", at, dm)
             s = fit(e, max(t, at + dm + wake), d)
             for m in (at, s - wake - dm):
-                ms = [m]
-                if len(o["mms"]) == 2:
-                    ms = [max([x - dm for x in [m] + [a for a, _, _ in busy["P"] if a < m]
-                               if x - dm >= first and fit("P", x - dm, dm) == x - dm], default=None), m]
-                if ms[0] is None or fit("P", m, dm) != m:
+                if fit("P", m, dm) != m:
                     continue
-                for b in range(8):
-                    if fit(b, ms[0], s + d + wake - ms[0]) == ms[0]:
-                        return s, ms, b
+                tries = [[m]]
+                if len(o["mms"]) == 2:
+                    gaps = sorted({x - dm for x in [m] + [a for a, _, _ in busy["P"] if a < m]} | {fit("P", first, dm)})
+                    tries = [[x, m] for x in gaps if first <= x <= m - dm + 1e-9 and fit("P", x, dm) == x]
+                for ms in tries:
+                    idle = [(max([y for _, y, _ in busy[b] if y <= ms[0] + 1e-9], default=-1.0), b) for b in range(8)
+                            if fit(b, ms[0], s + d + wake - ms[0]) == ms[0]]
+                    if idle:
+                        return s, ms, min(idle)[1]
             at = min([x[1] for b in range(8) for x in busy[b] if x[1] > at] + [at + dm])
 
     while ready:

from concourse.mybir import dt, AluOpType, ActivationFunctionType

C, E, B, R = 320, 20, 112, 2
L = C + B
K = 15
CHUNK = ((0, 6), (6, 12), (12, 15))
SUB = ((3, 3, 1), (3, 2, 2))
PIECE = (((0, 0, 132), (132, 132, 260), (192, 260, C)), ((0, 0, 188), (188, 188, C)))
ZN = ((0, 24, 38, 58, 80), (0, 6, 10, 28, 36, 46, 60, 70, 80))
ZT = ((-1, 19, 33, 43, 49, 65, 75, 80), (-1, 7, 33, 47, 53, 59, 65, 80))
LI = ((0, 10, 25, 40, 70, 85), (0, 10, 40, 70, 85))
AHEAD = 1.2
HEAD = 128
PAD = 4 * E
TG2, TRR, TW = 32, 192, 384
Q4, U8, F32, BF, I32, U16 = "float8_e4m3fn_x4", "uint8", "float32", "bfloat16", "int32", "uint16"

SCRATCH = {}
for _n, _w, _d in (("xin", 4 * C, BF), ("uin", 512, BF), ("vin", 512, BF), ("sti", 2, I32), ("wq", 512, Q4),
                   ("wp", 512, U8), ("uq", 128, Q4), ("up", 128, U8), ("urq", 256, Q4), ("urp", 256, U8),
                   ("nq", 128, Q4), ("npl", 128, U8), ("ones", 516, BF), ("ef", 516, BF), ("eq", 512, Q4),
                   ("ep", 512, U8), ("pi", 2, I32), ("ai", 8, I32), ("af", 24, F32), ("count", 40, F32),
                   ("wpen", 40, F32), ("lf", 48, F32), ("upo", 16, U16), ("off", 24, U16), ("items", 128, F32),
                   ("il", 256, F32), ("it", 256, F32), ("lam", 8, U16), ("kli", 6, I32), ("klf", 6, F32),
                   ("kl", 6, U16), ("kt", 192, BF), ("rst", 96, F32), ("rs2", 192, BF), ("stf", 2, F32),
                   ("bb", 64, F32), ("bt", 256, F32), ("bs", 32, F32), ("db", 32, F32), ("po", 32, U16),
                   ("bc0", 120, F32), ("cc", 8, F32), ("nn", 32, U16),
                   ("tp", 64 * K, F32), ("tb", 64 * K, F32), ("dd", 64 * K, F32), ("aa", 64 * K, F32),
                   ("s1", 64 * K, F32), ("pm", 256, F32), ("nr", 32 * K, BF), ("s3", 3 * 224, BF),
                   ("bc", 32 * K, BF), ("tt", 3 * TW, BF), ("ch", 96, U16), ("zn", 4 * C + 16, F32),
                   ("pout", 32, F32), ("ysb", C, F32), ("vq2", C, Q4), ("vp2", C, U8)):
    SCRATCH[_n] = ("sbuf", [128, _w], _d)
for _t in range(R):
    for _n, _w, _d in (("vq", 512, Q4), ("vp", 512, U8), ("lq", 512, Q4), ("lp", 512, U8), ("sc", 2 * L, F32),
                       ("dv", PAD + 4 * L, F32), ("tl", 128, U16), ("pen", 64 * K, BF), ("base", 96, F32),
                       ("wv", 96, F32), ("li", 96, U16), ("zt", 4 * C + 16, BF), ("zq", 388, Q4), ("zp", 388, U8),
                       ("ht", 4 * C, BF), ("hq", 388, Q4), ("hp", 388, U8), ("xt", 4 * C, BF)):
        SCRATCH["%s%d" % (_n, _t)] = ("sbuf", [128, _w], _d)
for _b in range(8):
    SCRATCH["ps%d" % _b] = ("psum", [128, 512], F32)
SEMAPHORES = ["cV", "cS", "cP", "cG", "sent", "win0", "win1", "lay0", "lay1"] + ["d%d" % i for i in range(24)]

ALU, ACT = AluOpType, ActivationFunctionType


def build(g, T, topo, core):
    ops, bank, tag, behind = [], {}, [""], [[]]
    cores, rank = T.cores, T.rank_of(core)
    n_r = len(cores)
    queue = {"S": g.scalar, "Y": g.sync}

    def ap(r):
        t = T["ps%d" % bank[r[0]]] if r[0][0] == "@" else T[r[0]]
        return t[:, r[1]:r[2]] if len(r) == 3 else t[:, r[1]:r[2]:r[3]]

    def cnt(r):
        return len(range(*r[1:]))

    def dtype(r):
        return F32 if r[0][0] == "@" else SCRATCH[r[0]][2]

    def add(on, size, reads, writes, emit, **kw):
        o = dict(on=on, size=size, reads=[x for x in reads if isinstance(x, tuple)], writes=writes, emit=emit,
                 after=list(behind[0]), kind="op", mms=[], tag=tag[0])
        o.update(kw)
        ops.append(o)
        return len(ops) - 1

    def kind(ind, o, *rs):
        two = all(dtype(r) in (BF, U16) for r in (o,) + rs)
        return ("pick" if ind else "half" if two else "one", cnt(o))

    def src(i, ind):
        return ap(i) if ind is None else ap(i).indirect(ap(ind))

    def scal(s):
        return ap(s) if isinstance(s, tuple) else s

    def copy(o, i, ind=None, scale=None, bias=None, on="SV", **more):
        whole = dtype(o) in (U16, I32) or dtype(i) in (U16, I32)

        def emit(e):
            if e == "S":
                kw = {}
                if scale is not None:
                    kw["scale"] = scal(scale)
                if bias is not None:
                    kw["bias"] = scal(bias)
                return g.scalar.activation(ap(o), src(i, ind), ACT.Copy if bias is None else ACT.Identity, **kw)
            if scale is None and bias is None:
                return g.vector.tensor_copy(ap(o), src(i, ind))
            if bias is None:
                return g.vector.tensor_scalar(ap(o), src(i, ind), scal(scale), None, ALU.mult)
            if scale is None:
                return g.vector.tensor_scalar(ap(o), src(i, ind), scal(bias), None, ALU.add)
            return g.vector.tensor_scalar(ap(o), src(i, ind), scal(scale), scal(bias), ALU.mult, ALU.add)
        return add("V" if whole else on, kind(ind, o, i), [i, ind, scale, bias], [o], emit, **more)

    def absol(o, i):
        return add("S", kind(None, o, i), [i], [o], lambda e: g.scalar.activation(ap(o), ap(i), ACT.Abs))

    def ts(o, i, s1, op0, s2=None, op1=None, ind=None):
        def emit(e):
            if op1 is None:
                return g.vector.tensor_scalar(ap(o), src(i, ind), scal(s1), None, op0)
            return g.vector.tensor_scalar(ap(o), src(i, ind), scal(s1), scal(s2), op0, op1)
        return add("V", kind(ind, o, i), [i, ind, s1, s2], [o], emit)

    def tt(o, a, b, op, ind=None):
        return add("V", ("pick" if ind else "two", cnt(o)), [a, b, ind], [o],
                   lambda e: g.vector.tensor_tensor(ap(o), src(a, ind), ap(b), op))

    def scan(o, a, b, op0, op1):
        return add("V", kind(None, o, a, b), [a, b], [o],
                   lambda e: g.vector.tensor_tensor_scan(ap(o), ap(a), ap(b), 0.0, op0, op1))

    def turn(o, i):
        return add("V", kind(None, o, i), [i], [o], lambda e: g.vector.transpose(ap(o), ap(i)))

    def fill(o, c):
        return add("V", kind(None, o), [], [o], lambda e: g.vector.memset(ap(o), c))

    def iota(o, pat, base, cm=0):
        def emit(e):
            if dtype(o) == I32:
                return g.iota(ap(o), pat, base, cm)
            return g.iota(ap(o), pat, base, cm, allow_small_or_imprecise_dtypes=True)
        return add("G", ("pool", cnt(o)), [], [o], emit)

    def quant(q, a, i):
        b = a + cnt(i) // 4
        c, p = (q[0], a, b), (q[1], a, b)
        return add("V", ("quant", cnt(i)), [i], [c, p], lambda e: g.vector.quantize_mx(ap(c), ap(p), ap(i)))

    named = [0]

    def product(o, terms, a, b, keep, scale=None):
        named[0] += 1
        ps, mms = ("@%d" % named[0], 0, b - a), []
        for i, (w, wa, x) in enumerate(terms):
            r = [(w[0], wa, wa + 128), (w[1], wa, wa + 128), (x[0], a, b), (x[1], a, b)]

            def emit(e, r=r, i=i):
                return g.tensor.matmul_mx(ap(ps), ap(r[0]), ap(r[1]), ap(r[2]), ap(r[3]), i == 0, i + 1 == len(terms))
            mms.append(add("P", ("mm", b - a), r, [ps], emit, kind="mm", acc=i > 0))
        return copy(o, (ps[0], keep, keep + cnt(o)), scale=scale, mms=mms)

    ndma = [0]

    def dma(out, in_, reads, writes, size):
        ndma[0] += 1
        return add("YS", ("dma", size), reads, writes, lambda e: queue[e].dma_start(out, in_),
                   kind="dma", sem="d%d" % (ndma[0] - 1))

    def u8(r):
        return ap(r).bitcast(dt.uint8)

    sends = []

    def send(step, s, d, sem):
        dst = cores[(rank - step) % n_r]
        rid, pid, _ = topo.addr(dst)
        codes = dtype(s) == Q4
        sends.append(add("G", ("send", cnt(s) * (4 if codes else 1)), [s], [],
                         lambda e: g.remote_dma(u8(d) if codes else ap(d), u8(s) if codes else ap(s), T.sem[sem],
                                                T.sem.sent, pid, rid, topo.mask(core, dst)),
                         kind="send", inc=len(topo.engines(core, dst)), after=sends[-1:]))

    def arrival(step, lands, sem, calls):
        add("A", ("arrive", 0), [], lands, None, kind="arrive", sem=sem, after=sends[-1:],
            inc=calls * len(topo.engines(cores[(rank + step) % n_r], core)))

    a0 = 4 * 128
    for i, j in enumerate((dma(T.wp[:, 0:HEAD], T.ws[:, 0:HEAD], [], [("wp", 0, HEAD)], HEAD),
                           dma(T.sti[:], T.st[:], [], [("sti", 0, 2)], 8),
                           dma(T.xin[:, 0:a0], T.x[:, 0:a0], [], [("xin", 0, a0)], 2 * a0),
                           dma(T.uin[:], T.u[:], [], [("uin", 0, 512)], 1024),
                           dma(T.xin[:, a0:4 * C], T.x[:, a0:4 * C], [], [("xin", a0, 4 * C)], 8 * C - 2 * a0))):
        ops[j]["extra"] = 5.0 - i

    iota(("pi", 0, 1), [[0, 1]], 0, 1)
    for j, m in enumerate((15, 16, 1)):
        ts(("ai", j, j + 1), ("pi", 0, 1), m, ALU.bitwise_and)
    copy(("af", 0, 3), ("ai", 0, 3))
    col = lambda j: ("af", j, j + 1)
    c_r, c_h, c_lh, c_tl, c_it, c_kl, c_1, c_2, c_al, c_be, c_x, c_y, c_nn = map(col, [0, 1] + list(range(5, 16)))
    copy(c_lh, c_h, scale=L / 16.0)
    copy(c_tl, c_r, scale=-1.0, bias=E + 15.0)
    copy(c_it, col(2), scale=63.0, bias=c_r)
    copy(c_kl, c_r, scale=0.2, bias=0.6)
    ts(c_1, c_r, 5.0, ALU.is_ge)
    ts(c_2, c_r, 10.0, ALU.is_ge)
    copy(c_x, c_h, scale=-1.0, bias=float(TG2 - TRR))
    copy(c_y, c_x, scale=c_1, bias=c_h)
    copy(c_al, c_2, scale=-float(TG2), bias=c_y)
    copy(c_be, c_2, scale=-80.0, bias=96.0)
    copy(c_nn, c_h, bias=32.0)
    iota(("cc", 0, 4), [[0, 2], [-1, 2]], 1)
    iota(("cc", 4, 8), [[0, 2], [-96, 2]], TRR - 64)
    copy(("cc", 0, 4), ("cc", 0, 4), scale=c_be, bias=c_al)
    tt(("cc", 0, 4), ("cc", 0, 4), ("cc", 4, 8), ALU.add)
    IL, FO, BO = 0, 16, 18
    copy(("off", FO, FO + 1), c_al, bias=TRR + 15.0)
    copy(("off", BO, BO + 1), c_r, bias=c_h)
    iota(("lf", 0, 16), [[16, 2], [32, 4], [0, 2]], 0)
    copy(("upo", 0, 16), ("lf", 0, 16))
    iota(("items", 0, 48), [[6, 2], [64, 4], [1, 6]], 0)
    iota(("items", 48, 60), [[64, 4], [1, 3]], 12)
    fill(("items", 60, 64), 0.0)
    copy(("items", 64, 128), ("items", 0, 64), bias=16.0)
    iota(("lf", 16, 24), [[16, 4], [1, 2]], 0)
    iota(("lf", 24, 32), [[16, 4], [64, 2]], 0)
    copy(("off", IL, IL + 8), ("lf", 16, 24), bias=c_it)
    copy(("off", IL + 8, IL + 16), ("lf", 24, 32), bias=c_r)
    copy(("il", 0, 256), ("items", 0, 128), ind=("off", IL, IL + 16))
    turn(("it", 0, 256), ("il", 0, 256))
    copy(("lam", 0, 4), ("it", 0, 128, 32))
    copy(("lam", 4, 8), ("it", 128, 256, 32), bias=1.0)
    iota(("count", 0, 40), [[1, 40]], 0)
    ts(("wpen", 0, 40), ("count", 0, 40), c_r, ALU.add, E + 15.0, ALU.is_equal)
    fill(("ones", 0, 516), 1.0)
    iota(("kt", 0, 192), [[32, 6], [-1, 16], [-256, 2]], 15)
    fill(("rst", 0, 96), 0.0)
    fill(("rst", 0, 96, 16), 1e29)
    fill(("rs2", 0, 192), 0.0)
    fill(("rs2", 0, 192, 32), 1e29)
    for q, (a, b) in enumerate(CHUNK):
        copy(("nr", 32 * a + 1, 32 * b, 2), ("ones", 0, 16 * (b - a)))
        fill(("s3", 224 * q + 32 * (b - a), 224 * q + 32 * (b - a) + 32), 255.0)
    fill(("tt", 2 * TW, 2 * TW + TRR), 0.0)
    fill(("pm", 0, 1), 0.0)
    fill(("zn", 0, 16), 0.0)
    copy(("klf", 0, 5), ("count", 0, 5), scale=3.2, bias=c_kl)
    copy(("kli", 0, 5), ("klf", 0, 5))
    ts(("kl", 0, 5), ("kli", 0, 5), 15.0, ALU.min, c_h, ALU.add)
    iota(("bc0", 0, 90), [[0, 3], [32, 6], [4, 5]], E + 15)
    copy(("bc0", 0, 80), ("bc0", 0, 80), scale=-1.0, bias=c_lh)
    add("G", ("pool", 516), [("ones", 0, 516)], [("ef", 0, 516)],
        lambda e: g.affine_select(T.ef[:, 0:516], T.ones[:, 0:516], [[-1, 516]], ALU.is_equal, 0.0, 3, 4))
    for b in range(4):
        quant(("eq", "ep"), 128 * b, ("ef", 3 - b, 515 - b))
    quant(("uq", "up"), 0, ("uin", 0, 512))
    add("V", ("pick", 256), [("uq", 0, 128), ("upo", 0, 16)], [("urq", 0, 256)],
        lambda e: g.vector.tensor_copy(T.urq[:, 0:256].bitcast(dt.uint32),
                                       T.uq[:, 0:128].bitcast(dt.uint32).indirect(T.upo[:, 0:16])))
    add("S", ("pick", 256), [("up", 0, 128), ("upo", 0, 16)], [("urp", 0, 256)],
        lambda e: g.scalar.activation(T.urp[:, 0:256], T.up[:, 0:128].indirect(T.upo[:, 0:16]), ACT.Copy))
    copy(("stf", 0, 2), ("sti", 0, 2), bias=c_lh)
    for t in range(R):
        copy(("bb", 32 * t, 32 * t + 32), ("count", 0, 32), scale=0.0, bias=("stf", t, t + 1))
    turn(("bt", 0, 64), ("bb", 0, 64))
    for e in range(1, 4):
        copy(("bt", 64 * e, 64 * e + 64), ("bt", 0, 64), bias=5.0 * e)

    def lists(t):
        s, bs = str(t), 16 * t
        copy(("tl" + s, 0, 64), ("bt", 32 * t, 256), ind=("lam", 0, 4), bias=c_tl)
        copy(("tl" + s, 64, 128), ("bt", 32 * t, 256), ind=("lam", 4, 8), bias=c_r)
        copy(("bs", bs, bs + 16), ("bt", 32 * t, 32 * t + 32), ind=("off", BO, BO + 1))
        tt(("db", bs, bs + K), ("bs", bs + 1, bs + 16), ("bs", bs, bs + K), ALU.subtract)
        copy(("db", bs, bs + K), ("db", bs, bs + K), bias=c_r)
        ts(("po", bs, bs + K), ("db", bs, bs + K), 0.0, ALU.max, E + 16.0, ALU.min)
        for e in range(3):
            copy(("pen" + s, e, 64 * K, 4), ("ones", 0, 16 * K), scale=0.0 if e else -1e29)
        copy(("pen" + s, 3, 64 * K, 4), ("wpen", 0, 40), ind=("po", bs, bs + K), scale=1e28)
        tt(("base" + s, 0, 80), ("bt", 32 * t, 32 * t + 32), ("bc0", 0, 80), ALU.subtract, ind=("kl", 0, 5))
        copy(("db", bs + K, bs + 16), ("bs", bs, bs + 1), scale=-1.0, bias=c_lh)
        copy(("wv" + s, 0, 10), ("count", 0, 10), scale=-4.0, bias=("db", bs + K, bs + 16))
        copy(("li" + s, 0, 10), ("wv" + s, 0, 10), scale=-4.0, bias=c_r)
        copy(("dv" + s, 0, PAD), ("ones", 0, PAD), scale=0.0)

    def window(t):
        s = str(t)
        head = HEAD if t == 0 else 0
        if head:
            send(1, ("wp", 0, head), ("lp0", 0, head), "lay0")
        send(1, ("vq" + s, B, 2 * B), ("vq" + s, 0, B), "win" + s)
        send(1, ("vp" + s, B, 2 * B), ("vp" + s, 0, B), "win" + s)
        arrival(1, [("vq" + s, 0, B), ("vp" + s, 0, B)], "win" + s, 2)

    def layer(t):
        s = str(t)
        head = HEAD if t == 0 else 0
        if head:
            dma(T.wp[:, HEAD:512], T.ws[:, HEAD:512], [("urq", 0, 1)], [("wp", HEAD, 512)], 512 - HEAD)
            dma(u8(("wq", 0, 512)), T.wc[:], [("urq", 0, 1)], [("wq", 0, 512)], 2048)
        send(1 + t, ("wp", head, 512), ("lp" + s, head, 512), "lay" + s)
        send(1 + t, ("wq", 0, 512), ("lq" + s, 0, 512), "lay" + s)
        arrival(1 + t, [("lq" + s, 0, 512), ("lp" + s, 0, 512)], "lay" + s, 3 if head else 2)
        if head:
            dma(T.vin[:], T.v[:], [("lq0", 0, 1)], [("vin", 0, 512)], 1024)

    EB = ("eq", "ep")

    def unpack(t, a, b, keep, x, n):
        V = ("vq%d" % t, "vp%d" % t)
        for h in range(2):
            product(("sc%d" % t, L * h + x, L * h + x + n), [(("urq", "urp"), 128 * h, V)], a, b, keep)
        for bb in range(4):
            product(("dv%d" % t, PAD + 4 * x + bb, PAD + 4 * (x + n), 4), [(EB, 128 * bb, V)], a, b, keep, 0.5)

    lists(0)
    quant(("vq0", "vp0"), B, ("xin", 0, a0))
    window(0)
    quant(("vq0", "vp0"), B + 128, ("xin", a0, 4 * C))
    unpack(0, B, L, 0, 0, C)
    layer(0)
    for t in range(R):
        s, s2 = str(t), str(t + 1)
        Z, H, X = ("zq" + s, "zp" + s), ("hq" + s, "hp" + s), ("vq" + s2, "vp" + s2)
        tag[0] = s + "n"
        unpack(t, 0, 128, 0, C, B)
        win, wv, li = ("sc" + s, 0, 2 * L), "wv" + s, "li" + s
        state = ("off", FO, FO + 1)
        for q, (a, b) in enumerate(CHUNK):
            n, tab, s3 = b - a, TW * q, 224 * q
            tag[0] = s + "c" + str(q)
            for i in range(SUB[t][q]):
                c, d = 4 * a + 4 * n * i // SUB[t][q], 4 * a + 4 * n * (i + 1) // SUB[t][q]
                tp, tb, dd = [(x, 16 * c, 16 * d) for x in ("tp", "tb", "dd")]
                copy(tp, win, ind=("tl" + s, c, d))
                turn(tb, tp)
                tt(dd, win, tb, ALU.subtract, ind=("tl" + s, 64 + c, 64 + d))
            for e in range(4):
                absol(("aa", 64 * a + e, 64 * b, 4), ("dd", 64 * a + 16 * n * e, 64 * a + 16 * n * (e + 1)))
            scan(("s1", 64 * a, 64 * b), ("pen" + s, 64 * a, 64 * b), ("aa", 64 * a, 64 * b), ALU.add, ALU.max)
            dist = ("s1", 64 * a + 3, 64 * b, 4)
            scan(("pm", 16 * a + 1, 16 * b + 1), ("rst", 0, 16 * n), dist, ALU.max, ALU.min)
            tt(("nr", 32 * a, 32 * b, 2), dist, ("pm", 16 * a, 16 * b), ALU.is_ge)
            scan(("s3", s3, s3 + 32 * n), ("nr", 32 * a, 32 * b), ("kt", 0, 32 * n), ALU.mult, ALU.max)
            scan(("bc", 32 * a, 32 * b), ("rs2", 0, 32 * n), ("s3", s3 + 31, s3 + 31 + 32 * n), ALU.max, ALU.min)
            rr = ("tt", tab + TRR, tab + TRR + 32 * n)
            turn(rr, ("bc", 32 * a, 32 * b))
            g2 = ("tt", tab + TG2, tab + TG2 + 32 * (n - 1))
            copy(("nn", 2 * a, 2 * b - 2), ("bc", 32 * a, 32 * b - 32, 16), bias=c_nn)
            copy(g2, rr, ind=("nn", 2 * a, 2 * b - 2))
            for i in range(n // 3):
                copy(("tt", tab + 16 * i, tab + 16 * i + 16), g2, ind=("nn", 2 * a + 6 * i, 2 * a + 6 * i + 1))
            for i in range(a // 3, b // 3):
                tabs = ("tt", tab, tab + TRR + 32 * n)
                now = state
                if 3 * i + 3 < K:
                    ts(("ch", 16 * i, 16 * i + 16), tabs, ("cc", i, i + 1), ALU.add, ind=now)
                    state = ("ch", 16 * i + 10, 16 * i + 11)
                tt((wv, 10 + 15 * i, 26 + 15 * i), tabs, ("base" + s, 15 * i, 15 * i + 16), ALU.subtract, ind=now)
        part = lambda c: s + str(sum(4 * c >= x[2] for x in PIECE[t][:-1]))
        for c, d in zip(LI[t][1:], LI[t][2:]):
            tag[0] = part(c - 5)
            copy((li, c, d), (wv, c, d), scale=-4.0, bias=c_r)
        for c, d in zip(ZN[t], ZN[t][1:]):
            tag[0] = part(c)
            copy(("zn", 16 * c + 16, 16 * d + 16), ("dv" + s, PAD, PAD + 4 * L), ind=(li, c, d))
        for c, d in zip(ZT[t], ZT[t][1:]):
            tag[0] = part(c)
            tt(("zt" + s, 16 * c + 16, 16 * d + 16), ("dv" + s, 0, PAD + 4 * L), ("zn", 16 * c + 16, 16 * d + 16),
               ALU.add, ind=(li, c + 5, d + 5))
        copy(("pout", 16 * t, 16 * t + 16), (wv, 5, 85, 5), scale=-1.0, bias=-float(E))
        end = 0
        for i, (a, new, b) in enumerate(PIECE[t]):
            at, end = end, end + b - a
            tag[0] = s + str(i)
            j = quant(Z, at, ("zt" + s, 4 * a + 16, 4 * b + 16))
            if b == C and t + 1 < R:
                behind[0], tag[0] = [j], ""
                lists(t + 1)
                quant(("nq", "npl"), 0, ("vin", 0, 512))
                behind[0], tag[0] = [], s + str(i)
            for bb in range(4):
                product(("ht" + s, 4 * new + bb, 4 * b, 4), [(("lq" + s, "lp" + s), 128 * bb, Z)], at, end, new - a,
                        0.03125)
            quant(H, at, ("ht" + s, 4 * a, 4 * b))
            for bb in range(4):
                j = product(("xt" + s, 4 * new + bb, 4 * b, 4), [(EB, 128 * bb, Z), (EB, 128 * bb, H)], at, end, new - a)
                ops[j]["extra"] = AHEAD * (len(PIECE[t]) - 1 - i)
            if t + 1 < R:
                quant(X, B + at, ("xt" + s, 4 * a, 4 * b))
                if i == 0:
                    window(t + 1)
                    layer(t + 1)
                unpack(t + 1, B + at, B + end, new - a, new, b - new)
            else:
                quant(X, a, ("xt" + s, 4 * a, 4 * b))
                keep = PIECE[t][i + 1][0] if i + 1 < len(PIECE[t]) else b
                dma(T.oc[:, 4 * a:4 * keep], u8(("vq2", a, keep)), [("vq2", a, keep)], [], 4 * (keep - a))
                product(("ysb", new, b), [(("nq", "npl"), 0, X)], a, b, new - a)
                dma(T.y[:, new:b], T.ysb[:, new:b], [("ysb", new, b)], [], 4 * (b - new))
    dma(T.ol[:], T.pout[0:128:16, 0:32], [("pout", 0, 32)], [], 8)
    for k in range(4):
        dma(T.osc[4 * k:4 * k + 4, 0:C], T.vp2[32 * k:32 * k + 4, 0:C], [("vp2", 0, C)], [], 10)
    return ops, bank


def depend(ops):
    seen = {}
    for i, o in enumerate(ops):
        deps = {}
        for wr, rs in ((False, o["reads"]), (True, o["writes"])):
            for r in rs:
                cols = set(range(*r[1:]))
                for j, w, c in seen.get(r[0], []):
                    if j != i and (wr or w) and not cols.isdisjoint(c):
                        deps[j] = not (r[0][0] == "@" and o.get("acc"))
                seen.setdefault(r[0], []).append((i, wr, cols))
        for j in o["after"]:
            deps.setdefault(j, False)
        o["deps"] = deps


NOMINAL = dict(cycle=1.05e-3, pick=1.56, wake=0.2, pe=0.6e-3, dma=1.2, issue=0.15, local=180e3, first=1.0,
               remote=0.7, link=100e3, lean=0.6)
LEAN = {"": 0, "tp": 0, "tt": 0.2, "dv": 0.05, "ht11": 0, "xt00": 0.05, "xt11": 0}
BUMP = {"eq": -2, "kt": -1, "sc": -0.25, "tp": 1, "tb": 0.5, "aa": -0.5, "wv": -1,
        "0n": -1, "0c0": -1, "tt0c1": -2, "tp0c2": -0.25, "dd0c2": 0.25, "xt01": 2, "02": 0.5,
        "tt1c0": -1, "tp1c1": -1, "1c2": 0.25, "tp1c2": -2, "zn10": -1, "ht10": -2}
GAP = {"0c0": 0.25, "0c2": 0.25, "00": 0.25, "02": 0.25, "1c0": 0.25, "1c1": 0.3, "1c2": 0.3, "10": 0.16, "11": 0.16}


def cost(o, e, P):
    k, n = o["size"]
    c = P["cycle"]
    if k == "pick":
        return (60 if e == "V" else 78) * c + n * P["pick"] * c
    if k in ("half", "one", "two"):
        return max(64, n * (2 if k == "two" else 0.5 if k == "half" and e == "V" else 1)) * c
    if k == "quant":
        return (15 + 0.265 * n) * c
    if k == "mm":
        return (n + 16) * P["pe"]
    if k == "pool":
        return (180 + 2 * n) * c
    return P["issue"] if k != "arrive" else 0.0


def place(ops, bank, P=NOMINAL, rank=None):
    wake = P["wake"]

    def name(o):
        return o["writes"][0][0][:2] if o["kind"] == "op" else ""

    def tail(o):
        k, n = o["size"]
        return P["dma"] + 128 * n / P["local"] if k == "dma" else P["remote"] + 128 * n / P["link"] if k == "send" else 0.0

    for o in ops:
        o["rest"], o["end"], o["users"] = 0.0, None, []
    for o in reversed(ops):
        o["rest"] += cost(o, o["on"][0], P) + tail(o) + o.get("extra", 0.0)
        for j, hard in o["deps"].items():
            gap = wake if hard else -tail(ops[j]) if o["kind"] != "arrive" else 0.0
            ops[j]["rest"] = max(ops[j]["rest"], o["rest"] + gap)
    need = {}
    for i, o in enumerate(ops):
        if o["kind"] != "mm":
            need[i] = {j for m in o["mms"] + [i] for j in ops[m]["deps"]} - set(o["mms"])
            for j in need[i]:
                ops[j]["users"].append(i)
    rank = rank or {i: -ops[i]["rest"] - BUMP.get(ops[i]["tag"], 0.0)
                    - BUMP.get(name(ops[i]) + ops[i]["tag"], BUMP.get(name(ops[i]), 0.0)) for i in need}
    ready = [i for i in need if not need[i]]
    busy = {e: [] for e in list("VSPGYA") + list(range(8))}
    link, plan = [0.0, P["first"]], []

    def after(o):
        t = 0.0
        for j, hard in o["deps"].items():
            if ops[j]["end"] is not None:
                t = max(t, ops[j]["end"] + GAP.get(o["tag"], wake) if hard
                        else ops[j]["end" if o["kind"] == "arrive" else "issued"])
        return t

    def fit(e, t, d):
        for a, b, _ in busy[e]:
            if t + d <= a + 1e-9:
                break
            t = max(t, b)
        return t

    def hold(e, t, d, i):
        busy[e].append((t, t + d, i))
        busy[e].sort()

    def slot(o, e):
        d, t = cost(o, e, P) + (link[1] if o["kind"] == "send" else 0.0), after(o)
        if not o["mms"]:
            return fit(e, t, d), None, None
        dm, first = cost(ops[o["mms"][0]], "P", P), after(ops[o["mms"][0]])
        at = max(after(ops[o["mms"][-1]]), first + dm * (len(o["mms"]) - 1))
        while True:
            at = fit("P", at, dm)
            s = fit(e, max(t, at + dm + wake), d)
            for m in (at, s - wake - dm):
                if fit("P", m, dm) != m:
                    continue
                tries = [[m]]
                if len(o["mms"]) == 2:
                    gaps = sorted({x - dm for x in [m] + [a for a, _, _ in busy["P"] if a < m]} | {fit("P", first, dm)})
                    tries = [[x, m] for x in gaps if first <= x <= m - dm + 1e-9 and fit("P", x, dm) == x]
                for ms in tries:
                    idle = [(max([y for _, y, _ in busy[b] if y <= ms[0] + 1e-9], default=-1.0), b) for b in range(8)
                            if fit(b, ms[0], s + d + wake - ms[0]) == ms[0]]
                    if idle:
                        return s, ms, min(idle)[1]
            at = min([x[1] for b in range(8) for x in busy[b] if x[1] > at] + [at + dm])

    while ready:
        i = min(ready, key=lambda i: rank[i])
        o = ops[i]
        lean = LEAN.get(name(o) + o["tag"], LEAN.get(name(o), P["lean"]))
        _, e, (t, m, b) = min((x[0] + cost(o, e, P) + lean * k, e, x)
                              for k, e in enumerate(o["on"]) for x in [slot(o, e)])
        d = cost(o, e, P)
        if o["mms"]:
            bank[o["reads"][0][0]] = b
            hold(b, m[0], t + d + wake - m[0], i)
            for j, at in zip(o["mms"], m):
                hold("P", at, cost(ops[j], "P", P), j)
                plan.append((at, "P", j))
                ops[j]["end"] = ops[j]["issued"] = at + cost(ops[j], "P", P)
        if o["kind"] == "send":
            d, link[1] = d + link[1], 0.0
            link[0] = max(link[0], t + d) + tail(o) - P["remote"]
        o["issued"], o["end"] = t + d, link[0] + P["remote"] if o["kind"] == "send" else t + d + tail(o)
        hold(e, t, d, i)
        plan.append((t, e, i))
        ready.remove(i)
        for j in o["mms"] + [i]:
            for u in ops[j]["users"]:
                need[u].discard(j)
                if not need[u]:
                    ready.append(u)
    for b in range(8):
        for x, y in zip(busy[b], busy[b][1:]):
            ops[ops[y[2]]["mms"][0]]["deps"][x[2]] = True
    return [(e, i) for _, e, i in sorted(plan)]


def rank_program(g, core, T, topo):
    if T.rank_of(core) is None:
        return
    ops, bank = build(g, T, topo, core)
    depend(ops)
    plan = place(ops, bank)
    queue = {"V": g.vector, "S": g.scalar, "P": g.tensor, "G": g, "Y": g.sync}
    known = {e: {} for e in queue}
    count, waited = {}, {}
    for at, (e, i) in enumerate(plan):
        o = ops[i]
        o["at"] = at
        if o["kind"] == "arrive":
            o["mark"], o["clock"] = (o["sem"], o["inc"]), {o["sem"]: o["inc"]}
            count[o["sem"]] = o["inc"]
            continue
        for d in sorted([ops[j] for j, hard in o["deps"].items() if hard], key=lambda d: -d["at"]):
            sem, n = d["mark"]
            if known[e].get(sem, 0) < n:
                queue[e].wait_ge(T.sem[sem], n)
                waited[sem] = max(waited.get(sem, 0), n)
                for k, v in d["clock"].items():
                    known[e][k] = max(known[e].get(k, 0), v)
        ins = o["emit"](e)
        if o["kind"] == "send":
            count["sent"] = count.get("sent", 0) + o["inc"]
            continue
        sem, inc = (o["sem"], 16) if o["kind"] == "dma" else ("c" + e, 1)
        ins.then_inc(T.sem[sem], inc)
        count[sem] = count.get(sem, 0) + inc
        o["mark"], o["clock"] = (sem, count[sem]), dict(known[e])
        o["clock"][sem] = count[sem]
    for sem, n in count.items():
        if waited.get(sem, 0) < n:
            g.wait_ge(T.sem[sem], n)
